import numpy as np
import ml_dtypes


def mxq(x, axis, fmt="e4m3"):
    dtype, down = {"e4m3": (ml_dtypes.float8_e4m3fn, 7), "e5m2": (ml_dtypes.float8_e5m2, 14)}[fmt]
    v = np.moveaxis(np.asarray(x, np.float32).astype(ml_dtypes.bfloat16).astype(np.float64), axis, -1)
    blocks = v.reshape(v.shape[:-1] + (-1, 32))
    amax = np.abs(blocks).max(-1, keepdims=True)
    byte = np.maximum(np.where(amax > 0, np.frexp(amax)[1] - 1 + 127, 0) - down, 1)
    scale = np.exp2(byte - 127.0)
    codes = (blocks / scale).astype(np.float32).astype(dtype).astype(np.float64)
    return np.moveaxis((codes * scale).reshape(v.shape), -1, axis)


WIDE = False


def mx_kscale(k):
    if not WIDE:
        return np.ones(k)
    levels = np.array([10, -10, 5, -5, 0])
    if k % 512:
        return np.exp2(np.random.permutation(np.resize(levels, k // 32))).repeat(32)
    a = np.empty((k // 512, 16))
    for p in range(k // 512):
        a[p, :8] = np.random.permutation(np.resize(levels, 8))
        for g in range(8):
            far = levels[np.abs(levels - a[p, g]) >= 10]
            a[p, g + 8] = far[np.random.randint(len(far))]
    return np.exp2(a.ravel()).repeat(32)


def f64(x):
    return np.asarray(x).astype(np.float64)


def striped(idx):
    return np.tile(idx.reshape(-1, 16).T, (8, 1)).astype(np.uint16)


def unstriped(offs):
    return offs[:16].T.reshape(-1).astype(np.int64)


def silu(v):
    return v / (1.0 + np.exp(-np.maximum(v, -700.0)))


K, T, E, C, N = 1024, 512, 4, 256, 256


def by_expert(wq, xq):
    return np.concatenate([wq[e].T @ xq[:, e * C:(e + 1) * C] for e in range(E)], axis=1)


def setup_inputs():
    n = np.random.standard_normal
    s = mx_kscale(K)[:, None]
    first = np.random.permutation(np.repeat(np.arange(E), T // E))
    second = (first + 1 + np.random.permutation(np.repeat(np.arange(E - 1), -(-T // (E - 1)))[:T])) % E
    while np.bincount(second, minlength=E).max() != T // E:
        load = np.bincount(second, minlength=E); hi, lo = int(load.argmax()), int(load.argmin())
        t = np.flatnonzero((second == hi) & (first != lo))[0]; second[t] = lo
    slot_token = np.empty(E * C, np.int64); pos = np.empty((2, T), np.int64); fill = np.zeros(E, np.int64)
    place = np.stack([np.random.permutation(C) for _ in range(E)])
    for r, deal in enumerate((first, second)):
        for t in np.random.permutation(T):
            e = deal[t]; j = e * C + place[e, fill[e]]; fill[e] += 1; slot_token[j] = t; pos[r, t] = j
    g = np.random.uniform(0.2, 0.8, T)
    return {
        "xT": (n((K, T)) * s).astype(np.float32),
        "w": (n((E, K, N)) / np.sqrt(K) / s[None]).astype(np.float32),
        "b": (0.3 * n((N, E))).astype(np.float32),
        "gate": np.stack([np.tile(g, (N, 1)), np.tile(1.0 - g, (N, 1))]).astype(np.float32),
        "offs": striped(slot_token),
        "pos1": striped(pos[0]),
        "pos2": striped(pos[1]),
    }


def reference(xT, w, b, gate, offs, pos1, pos2):
    idx = unstriped(offs)
    xq = mxq(f64(xT)[:, idx], 0, "e4m3")
    y = by_expert(mxq(f64(w), 1, "e4m3"), xq)
    y = silu(y + np.repeat(f64(b), C, axis=1))
    return f64(gate[0]) * y[:, unstriped(pos1)] + f64(gate[1]) * y[:, unstriped(pos2)]

@@ -1,0 +1,187 @@
+import concourse.mybir as mybir
+from concourse.masks import make_identity
+
+K, T, E, C, N = 1024, 512, 4, 256, 256
+FLOPS = 2 * K * N * E * C
+
+F32 = mybir.dt.float32
+BF16 = mybir.dt.bfloat16
+I32 = mybir.dt.int32
+U32 = mybir.dt.uint32
+U16 = mybir.dt.uint16
+U8 = mybir.dt.uint8
+FP8X4 = mybir.dt.float8_e4m3fn_x4
+MULT, ADD = mybir.AluOpType.mult, mybir.AluOpType.add
+SILU = mybir.ActivationFunctionType.Silu
+
+P = 128
+PACK = 4
+K_PASS = P * PACK
+PASSES = K // K_PASS
+BLOCKS = N // P
+SLOTS = E * C
+HALF = T // 2
+WINDOW = 1376
+PE_COLS = 384
+
+
+def interleave(copy, out, in_):
+    copy(out.rearrange("p (c i) t -> p c t i", i=4), in_.rearrange("p t (c i) -> p c t i", i=4))
+
+
+def tile_routed_moe_kernel(tc, xT, w, b, gate, offs, pos1, pos2, out):
+    nc = tc.nc
+    with (
+        tc.tile_pool(name="lists", bufs=1) as lists,
+        tc.tile_pool(name="keep", bufs=1) as keep,
+        tc.psum_pool(name="psum", bufs=1) as psum,
+    ):
+        sc, ve, gp = nc.scalar.copy, nc.vector.tensor_copy, nc.gpsimd.tensor_copy
+        offs_sb = lists.tile([P, SLOTS // 16], U16, name="offs_sb")
+        pos_sb = [lists.tile([P, T // 16], U16, name=f"pos_sb{r}") for r in range(2)]
+        x_raw = [keep.tile([P, PACK, T], F32, name=f"x_raw{g}") for g in range(PASSES)]
+        w_raw = [keep.tile([P, PASSES, PACK, N], F32, name=f"w_raw{e}") for e in range(E)]
+        bias = keep.tile([P, BLOCKS, E], F32, name="bias")
+        gates = [keep.tile([P, 2, T], F32, name=f"gates{c}") for c in range(BLOCKS)]
+        x_scales = keep.tile([P, WINDOW], U8, name="x_scales", align_bytes=64)
+        nc.gpsimd.memset(x_scales[:], 0)
+        x_codes = [keep.tile([P, WINDOW], I32, name=f"x_codes{g}", align_bytes=64) for g in range(PASSES)]
+        for g in range(PASSES):
+            nc.vector.memset(x_codes[g][:, T:], 0)
+        warm = keep.tile([P, 1], F32, name="warm")
+        nc.gpsimd.memset(warm[:], 0.0)
+        warm_out = keep.tile([P, 1], F32, name="warm_out")
+        nc.scalar.activation(warm_out[:], warm[:], SILU)
+        identity = keep.tile([P, P], F32, name="identity")
+        make_identity(nc, identity[:])
+
+        x_dram = [xT[g * K_PASS : (g + 1) * K_PASS, :].rearrange("(p j) n -> p j n", j=PACK) for g in range(PASSES)]
+
+        def load_x(g, lo=0, hi=T):
+            nc.sync.dma_start(x_raw[g][:, :, lo:hi], x_dram[g][:, :, lo:hi])
+
+        def load_w(e, lo=0, hi=N):
+            for g in range(PASSES):
+                nc.sync.dma_start(w_raw[e][:, g, :, lo:hi], w[e, g * K_PASS : (g + 1) * K_PASS, lo:hi].rearrange("(p j) n -> p j n", j=PACK))
+
+        load_x(0)
+        nc.sync.dma_start(offs_sb[:], offs)
+        load_x(1)
+        load_w(0)
+        load_w(1)
+        load_w(2)
+        load_w(3)
+        nc.sync.dma_start(bias[:], b.rearrange("(c p) e -> p c e", p=P))
+        nc.sync.dma_start(pos_sb[0][:], pos1)
+        nc.sync.dma_start(pos_sb[1][:], pos2)
+        for c in range(BLOCKS):
+            nc.sync.dma_start(gates[c][:], gate[:, c * P : (c + 1) * P, :].rearrange("r p t -> p r t"))
+
+        slot_codes = [keep.tile([P, SLOTS], U32, name=f"slot_codes{g}", align_bytes=64) for g in range(PASSES)]
+        slot_scales = keep.tile([P, SLOTS], U8, name="slot_scales", align_bytes=64)
+
+        def prepare_x(g, lo, n, copy):
+            x_bf = keep.tile([P, n, PACK], BF16, name=f"x_bf{g}{lo}", align_bytes=64)
+            interleave(copy, x_bf[:], x_raw[g][:, :, lo : lo + n])
+            for a in range(0, n, 256):
+                m = min(256, n - a)
+                nc.vector.quantize_mx(
+                    out=x_codes[g][:, lo + a : lo + a + m].bitcast(FP8X4),
+                    scales=x_scales[4 * g :, lo + a : lo + a + m],
+                    in_=x_bf[:, a : a + m, :].rearrange("p n t -> p (n t)"),
+                )
+
+        prepare_x(0, 0, 256, ve)
+        prepare_x(0, 256, 256, sc)
+        nc.vector.tensor_copy(slot_codes[0][:], x_codes[0][:].bitcast(U32).indirect(offs_sb[:]))
+        prepare_x(1, 0, 256, sc)
+        prepare_x(1, 256, 256, sc)
+        nc.vector.tensor_copy(slot_codes[1][:], x_codes[1][:].bitcast(U32).indirect(offs_sb[:]))
+        nc.vector.tensor_copy(slot_scales[:], x_scales[:].indirect(offs_sb[:]))
+
+        y = [keep.tile([P, SLOTS], F32, name=f"y{c}") for c in range(BLOCKS)]
+        groups = {
+            0: [(3, 0)],
+            1: [(1, 1), (3, 1)],
+            2: [(2, 0), (1, 0)],
+            3: [(2, 1)],
+            4: [(0, 1), (0, 0)],
+        }
+        w_bf, w_codes, w_scales, w_to = {}, {}, {}, {}
+        for i, blocks in groups.items():
+            bf = keep.tile([P, len(blocks), PASSES, P, PACK], BF16, name=f"w_bf{i}", align_bytes=64)
+            codes = keep.tile([P, len(blocks), PASSES, P], U32, name=f"w_codes{i}", align_bytes=64)
+            scales = keep.tile([P, len(blocks), PASSES, P], U8, name=f"w_scales{i}", align_bytes=64)
+            w_bf[i] = (bf, codes, scales)
+            for j, ec in enumerate(blocks):
+                w_to[ec], w_codes[ec], w_scales[ec] = bf[:, j, :, :, :], codes[:, j, :, :], scales[:, j, :, :]
+
+        def copy_w(e, c, copy, whole):
+            to, cols = w_to[e, c], slice(c * P, (c + 1) * P)
+            if whole:
+                copy(to.rearrange("p g (c i) t -> p g c t i", i=4), w_raw[e][:, :, :, cols].rearrange("p g t (c i) -> p g c t i", i=4))
+            else:
+                for g in range(PASSES):
+                    interleave(copy, to[:, g, :, :], w_raw[e][:, g, :, cols])
+
+        def quantise_w(i):
+            bf, codes, scales = w_bf[i]
+            nc.vector.quantize_mx(
+                out=codes[:].rearrange("p b g n -> p (b g n)").bitcast(FP8X4),
+                scales=scales[:].rearrange("p b g n -> p (b g n)"),
+                in_=bf[:].rearrange("p b g n t -> p (b g n t)"),
+            )
+
+        def multiply(c):
+            for e in range(E):
+                slots = slice(e * C, (e + 1) * C)
+                acc = psum.tile([P, C], F32, name=f"acc{e}{c}")
+                for g in range(PASSES):
+                    nc.tensor.matmul_mx(
+                        out=acc[:],
+                        lhsT=w_codes[e, c][:, g, :].bitcast(FP8X4),
+                        lhsT_scale=w_scales[e, c][:, g, :],
+                        rhs=slot_codes[g][:, slots].bitcast(FP8X4),
+                        rhs_scale=slot_scales[4 * g :, slots],
+                        start=(g == 0),
+                        stop=(g == PASSES - 1),
+                    )
+                nc.scalar.activation(y[c][:, slots], acc[:], SILU, bias=bias[:, c, e : e + 1])
+
+        copy_w(0, 1, sc, True)
+        copy_w(0, 0, sc, True)
+        copy_w(2, 0, sc, False)
+        copy_w(1, 0, sc, True)
+        quantise_w(2)
+        quantise_w(4)
+        copy_w(3, 0, ve, False)
+        quantise_w(0)
+        copy_w(2, 1, ve, False)
+        copy_w(1, 1, sc, True)
+        copy_w(3, 1, sc, False)
+        quantise_w(1)
+        multiply(0)
+        quantise_w(3)
+        multiply(1)
+
+        def gather(c, r, lo=0, hi=T):
+            part = keep.tile([P, hi - lo], F32, name=f"part{c}{r}{lo}")
+            nc.vector.tensor_tensor(part[:], y[c][:].indirect(pos_sb[r][:, lo // 16 : hi // 16]), gates[c][:, r, lo:hi], MULT)
+            return part
+
+        total0_psum = psum.tile([P, PE_COLS], F32, name="acc00")
+        parts0 = []
+        for r in range(2):
+            parts0.append(gather(0, r))
+            nc.tensor.matmul(total0_psum[:], identity[:], parts0[r][:, :PE_COLS], start=(r == 0), stop=(r == 1))
+        total0 = keep.tile([P, T], F32, name="total0")
+        nc.scalar.copy(total0[:, :PE_COLS], total0_psum[:])
+
+        first = gather(1, 0)
+        nc.vector.tensor_tensor(total0[:, PE_COLS:], parts0[0][:, PE_COLS:], parts0[1][:, PE_COLS:], ADD)
+        nc.sync.dma_start(out[:P, :], total0[:])
+        seconds = [gather(1, 1, lo, lo + HALF) for lo in (0, HALF)]
+        for i, lo in enumerate((0, HALF)):
+            total1 = keep.tile([P, HALF], F32, name=f"total1{i}")
+            nc.vector.tensor_tensor(total1[:], first[:, lo : lo + HALF], seconds[i][:], ADD)
+            nc.sync.dma_start(out[P:, lo : lo + HALF], total1[:])

@@ -36,15 +36,16 @@ def tile_routed_moe_kernel(tc, xT, w, b, gate, offs, pos1, pos2, out):
         tc.tile_pool(name="keep", bufs=1) as keep,
         tc.psum_pool(name="psum", bufs=1) as psum,
     ):
-        sc, ve, gp = nc.scalar.copy, nc.vector.tensor_copy, nc.gpsimd.tensor_copy
+        sc, ve = nc.scalar.copy, nc.vector.tensor_copy
         offs_sb = lists.tile([P, SLOTS // 16], U16, name="offs_sb")
         pos_sb = [lists.tile([P, T // 16], U16, name=f"pos_sb{r}") for r in range(2)]
         x_raw = [keep.tile([P, PACK, T], F32, name=f"x_raw{g}") for g in range(PASSES)]
-        w_raw = [keep.tile([P, PASSES, PACK, N], F32, name=f"w_raw{e}") for e in range(E)]
+        w_raw = {(e, g): keep.tile([P, PACK, N], F32, name=f"w_raw{e}{g}") for e in range(E) for g in range(PASSES)}
         bias = keep.tile([P, BLOCKS, E], F32, name="bias")
-        gates = [keep.tile([P, 2, T], F32, name=f"gates{c}") for c in range(BLOCKS)]
+        gates = {(c, r): keep.tile([P, T], F32, name=f"gates{c}{r}") for c in range(BLOCKS) for r in range(2)}
+        nc.scalar.dma_start(bias[:], b.rearrange("(c p) e -> p c e", p=P))
         x_scales = keep.tile([P, WINDOW], U8, name="x_scales", align_bytes=64)
-        nc.gpsimd.memset(x_scales[:], 0)
+        nc.vector.memset(x_scales[:].bitcast(I32), 0)
         x_codes = [keep.tile([P, WINDOW], I32, name=f"x_codes{g}", align_bytes=64) for g in range(PASSES)]
         for g in range(PASSES):
             nc.vector.memset(x_codes[g][:, T:], 0)
@@ -55,118 +56,101 @@ def tile_routed_moe_kernel(tc, xT, w, b, gate, offs, pos1, pos2, out):
         identity = keep.tile([P, P], F32, name="identity")
         make_identity(nc, identity[:])
 
-        x_dram = [xT[g * K_PASS : (g + 1) * K_PASS, :].rearrange("(p j) n -> p j n", j=PACK) for g in range(PASSES)]
+        def rows(matrix, g):
+            return matrix[g * K_PASS : (g + 1) * K_PASS, :].rearrange("(p j) n -> p j n", j=PACK)
 
-        def load_x(g, lo=0, hi=T):
-            nc.sync.dma_start(x_raw[g][:, :, lo:hi], x_dram[g][:, :, lo:hi])
-
-        def load_w(e, lo=0, hi=N):
+        for g in range(PASSES):
+            for lo in (0, HALF):
+                nc.sync.dma_start(x_raw[g][:, :, lo : lo + HALF], rows(xT, g)[:, :, lo : lo + HALF])
+            if g == 0:
+                nc.sync.dma_start(offs_sb[:], offs)
+        for e in range(E):
             for g in range(PASSES):
-                nc.sync.dma_start(w_raw[e][:, g, :, lo:hi], w[e, g * K_PASS : (g + 1) * K_PASS, lo:hi].rearrange("(p j) n -> p j n", j=PACK))
-
-        load_x(0)
-        nc.sync.dma_start(offs_sb[:], offs)
-        load_x(1)
-        load_w(0)
-        load_w(1)
-        load_w(2)
-        load_w(3)
-        nc.sync.dma_start(bias[:], b.rearrange("(c p) e -> p c e", p=P))
+                nc.sync.dma_start(w_raw[e, g][:], rows(w[e], g))
         nc.sync.dma_start(pos_sb[0][:], pos1)
         nc.sync.dma_start(pos_sb[1][:], pos2)
         for c in range(BLOCKS):
-            nc.sync.dma_start(gates[c][:], gate[:, c * P : (c + 1) * P, :].rearrange("r p t -> p r t"))
+            for r in range(2):
+                nc.sync.dma_start(gates[c, r][:], gate[r, c * P : (c + 1) * P, :])
 
         slot_codes = [keep.tile([P, SLOTS], U32, name=f"slot_codes{g}", align_bytes=64) for g in range(PASSES)]
         slot_scales = keep.tile([P, SLOTS], U8, name="slot_scales", align_bytes=64)
 
-        def prepare_x(g, lo, n, copy):
-            x_bf = keep.tile([P, n, PACK], BF16, name=f"x_bf{g}{lo}", align_bytes=64)
-            interleave(copy, x_bf[:], x_raw[g][:, :, lo : lo + n])
-            for a in range(0, n, 256):
-                m = min(256, n - a)
-                nc.vector.quantize_mx(
-                    out=x_codes[g][:, lo + a : lo + a + m].bitcast(FP8X4),
-                    scales=x_scales[4 * g :, lo + a : lo + a + m],
-                    in_=x_bf[:, a : a + m, :].rearrange("p n t -> p (n t)"),
-                )
+        def prepare_x(g, lo, on_vector):
+            x_bf = keep.tile([P, HALF, PACK], BF16, name=f"x_bf{g}{lo}", align_bytes=64)
+            if on_vector > 0:
+                interleave(ve, x_bf[:, :on_vector, :], x_raw[g][:, :, lo : lo + on_vector])
+            if on_vector < HALF:
+                interleave(sc, x_bf[:, on_vector:, :], x_raw[g][:, :, lo + on_vector : lo + HALF])
+            nc.vector.quantize_mx(
+                out=x_codes[g][:, lo : lo + HALF].bitcast(FP8X4),
+                scales=x_scales[4 * g :, lo : lo + HALF],
+                in_=x_bf[:].rearrange("p n t -> p (n t)"),
+            )
 
-        prepare_x(0, 0, 256, ve)
-        prepare_x(0, 256, 256, sc)
+        prepare_x(0, 0, HALF)
+        prepare_x(0, HALF, 160)
         nc.vector.tensor_copy(slot_codes[0][:], x_codes[0][:].bitcast(U32).indirect(offs_sb[:]))
-        prepare_x(1, 0, 256, sc)
-        prepare_x(1, 256, 256, sc)
+        prepare_x(1, 0, 0)
+        prepare_x(1, HALF, 0)
         nc.vector.tensor_copy(slot_codes[1][:], x_codes[1][:].bitcast(U32).indirect(offs_sb[:]))
         nc.vector.tensor_copy(slot_scales[:], x_scales[:].indirect(offs_sb[:]))
 
         y = [keep.tile([P, SLOTS], F32, name=f"y{c}") for c in range(BLOCKS)]
-        groups = {
-            0: [(3, 0)],
-            1: [(1, 1), (3, 1)],
-            2: [(2, 0), (1, 0)],
-            3: [(2, 1)],
-            4: [(0, 1), (0, 0)],
-        }
-        w_bf, w_codes, w_scales, w_to = {}, {}, {}, {}
-        for i, blocks in groups.items():
-            bf = keep.tile([P, len(blocks), PASSES, P, PACK], BF16, name=f"w_bf{i}", align_bytes=64)
-            codes = keep.tile([P, len(blocks), PASSES, P], U32, name=f"w_codes{i}", align_bytes=64)
-            scales = keep.tile([P, len(blocks), PASSES, P], U8, name=f"w_scales{i}", align_bytes=64)
-            w_bf[i] = (bf, codes, scales)
-            for j, ec in enumerate(blocks):
-                w_to[ec], w_codes[ec], w_scales[ec] = bf[:, j, :, :, :], codes[:, j, :, :], scales[:, j, :, :]
+        w_bf = keep.tile([P, BLOCKS, E, PASSES, P, PACK], BF16, name="w_bf", align_bytes=64)
+        w_codes = keep.tile([P, BLOCKS, E * PASSES, P], U32, name="w_codes", align_bytes=64)
+        w_scales = keep.tile([P, BLOCKS, E * PASSES, P], U8, name="w_scales", align_bytes=64)
+        acc = {(e, c): psum.tile([P, C], F32, name=f"acc{e}{c}") for e in range(E) for c in range(BLOCKS)}
 
-        def copy_w(e, c, copy, whole):
-            to, cols = w_to[e, c], slice(c * P, (c + 1) * P)
-            if whole:
-                copy(to.rearrange("p g (c i) t -> p g c t i", i=4), w_raw[e][:, :, :, cols].rearrange("p g t (c i) -> p g c t i", i=4))
-            else:
-                for g in range(PASSES):
-                    interleave(copy, to[:, g, :, :], w_raw[e][:, g, :, cols])
-
-        def quantise_w(i):
-            bf, codes, scales = w_bf[i]
-            nc.vector.quantize_mx(
-                out=codes[:].rearrange("p b g n -> p (b g n)").bitcast(FP8X4),
-                scales=scales[:].rearrange("p b g n -> p (b g n)"),
-                in_=bf[:].rearrange("p b g n t -> p (b g n t)"),
+        def copy_both(copy, e, g):
+            copy(
+                w_bf[:, :, e, g, :, :].rearrange("p c (m i) t -> p c m t i", i=4),
+                w_raw[e, g][:].rearrange("p t (c m i) -> p c m t i", c=BLOCKS, i=4),
             )
 
-        def multiply(c):
-            for e in range(E):
-                slots = slice(e * C, (e + 1) * C)
-                acc = psum.tile([P, C], F32, name=f"acc{e}{c}")
-                for g in range(PASSES):
-                    nc.tensor.matmul_mx(
-                        out=acc[:],
-                        lhsT=w_codes[e, c][:, g, :].bitcast(FP8X4),
-                        lhsT_scale=w_scales[e, c][:, g, :],
-                        rhs=slot_codes[g][:, slots].bitcast(FP8X4),
-                        rhs_scale=slot_scales[4 * g :, slots],
-                        start=(g == 0),
-                        stop=(g == PASSES - 1),
-                    )
-                nc.scalar.activation(y[c][:, slots], acc[:], SILU, bias=bias[:, c, e : e + 1])
+        def copy_block(copy, e, g, c):
+            interleave(copy, w_bf[:, c, e, g, :, :], w_raw[e, g][:, :, c * P : (c + 1) * P])
 
-        copy_w(0, 1, sc, True)
-        copy_w(0, 0, sc, True)
-        copy_w(2, 0, sc, False)
-        copy_w(1, 0, sc, True)
-        quantise_w(2)
-        quantise_w(4)
-        copy_w(3, 0, ve, False)
-        quantise_w(0)
-        copy_w(2, 1, ve, False)
-        copy_w(1, 1, sc, True)
-        copy_w(3, 1, sc, False)
-        quantise_w(1)
-        multiply(0)
-        quantise_w(3)
-        multiply(1)
+        def multiply(c, first, last):
+            nc.vector.quantize_mx(
+                out=w_codes[:, c, first:last, :].rearrange("p a n -> p (a n)").bitcast(FP8X4),
+                scales=w_scales[:, c, first:last, :].rearrange("p a n -> p (a n)"),
+                in_=w_bf[:, c].rearrange("p e g n t -> p (e g) (n t)")[:, first:last, :].rearrange("p a m -> p (a m)"),
+            )
+            for piece in range(first, last):
+                e, g = divmod(piece, PASSES)
+                slots = slice(e * C, (e + 1) * C)
+                nc.tensor.matmul_mx(
+                    out=acc[e, c][:],
+                    lhsT=w_codes[:, c, piece, :].bitcast(FP8X4),
+                    lhsT_scale=w_scales[:, c, piece, :],
+                    rhs=slot_codes[g][:, slots].bitcast(FP8X4),
+                    rhs_scale=slot_scales[4 * g :, slots],
+                    start=(g == 0),
+                    stop=(g == PASSES - 1),
+                )
+                if g == PASSES - 1:
+                    nc.scalar.activation(y[c][:, slots], acc[e, c][:], SILU, bias=bias[:, c, e : e + 1])
+
+        for e, g in ((0, 0), (0, 1), (1, 0), (1, 1), (2, 0)):
+            copy_both(sc, e, g)
+        copy_block(sc, 2, 1, 0)
+        copy_block(sc, 3, 0, 0)
+        copy_block(ve, 3, 1, 0)
+        multiply(0, 0, 4)
+        multiply(0, 4, 6)
+        multiply(0, 6, 7)
+        multiply(0, 7, 8)
+        multiply(1, 0, 4)
+        copy_block(ve, 2, 1, 1)
+        multiply(1, 4, 6)
+        copy_block(ve, 3, 0, 1)
+        copy_block(sc, 3, 1, 1)
+        multiply(1, 6, 8)
 
         def gather(c, r, lo=0, hi=T):
             part = keep.tile([P, hi - lo], F32, name=f"part{c}{r}{lo}")
-            nc.vector.tensor_tensor(part[:], y[c][:].indirect(pos_sb[r][:, lo // 16 : hi // 16]), gates[c][:, r, lo:hi], MULT)
+            nc.vector.tensor_tensor(part[:], y[c][:].indirect(pos_sb[r][:, lo // 16 : hi // 16]), gates[c, r][:, lo:hi], MULT)
             return part
 
         total0_psum = psum.tile([P, PE_COLS], F32, name="acc00")

@@ -22,7 +22,7 @@ BLOCKS = N // P
 SLOTS = E * C
 HALF = T // 2
 WINDOW = 1376
-PE_COLS = 384
+PE_COLS = 256
 
 
 def interleave(copy, out, in_):
@@ -40,10 +40,9 @@ def tile_routed_moe_kernel(tc, xT, w, b, gate, offs, pos1, pos2, out):
         offs_sb = lists.tile([P, SLOTS // 16], U16, name="offs_sb")
         pos_sb = [lists.tile([P, T // 16], U16, name=f"pos_sb{r}") for r in range(2)]
         x_raw = [keep.tile([P, PACK, T], F32, name=f"x_raw{g}") for g in range(PASSES)]
-        w_raw = {(e, g): keep.tile([P, PACK, N], F32, name=f"w_raw{e}{g}") for e in range(E) for g in range(PASSES)}
-        bias = keep.tile([P, BLOCKS, E], F32, name="bias")
+        w_raw = [keep.tile([P, PASSES, PACK, N], F32, name=f"w_raw{e}") for e in range(E)]
+        bias = [keep.tile([P, E], F32, name=f"bias{c}") for c in range(BLOCKS)]
         gates = {(c, r): keep.tile([P, T], F32, name=f"gates{c}{r}") for c in range(BLOCKS) for r in range(2)}
-        nc.scalar.dma_start(bias[:], b.rearrange("(c p) e -> p c e", p=P))
         x_scales = keep.tile([P, WINDOW], U8, name="x_scales", align_bytes=64)
         nc.vector.memset(x_scales[:].bitcast(I32), 0)
         x_codes = [keep.tile([P, WINDOW], I32, name=f"x_codes{g}", align_bytes=64) for g in range(PASSES)]
@@ -59,21 +58,21 @@ def tile_routed_moe_kernel(tc, xT, w, b, gate, offs, pos1, pos2, out):
         def rows(matrix, g):
             return matrix[g * K_PASS : (g + 1) * K_PASS, :].rearrange("(p j) n -> p j n", j=PACK)
 
+        nc.sync.dma_start(x_raw[0][:], rows(xT, 0))
+        nc.sync.dma_start(offs_sb[:], offs)
+        nc.sync.dma_start(x_raw[1][:], rows(xT, 1))
         for g in range(PASSES):
-            for lo in (0, HALF):
-                nc.sync.dma_start(x_raw[g][:, :, lo : lo + HALF], rows(xT, g)[:, :, lo : lo + HALF])
-            if g == 0:
-                nc.sync.dma_start(offs_sb[:], offs)
-        for e in range(E):
-            for g in range(PASSES):
-                nc.sync.dma_start(w_raw[e, g][:], rows(w[e], g))
+            for e in range(E):
+                nc.sync.dma_start(w_raw[e][:, g], rows(w[e], g))
+        nc.sync.dma_start(bias[0][:], b[:P, :])
         nc.sync.dma_start(pos_sb[0][:], pos1)
+        nc.sync.dma_start(bias[1][:], b[P:, :])
         nc.sync.dma_start(pos_sb[1][:], pos2)
         for c in range(BLOCKS):
             for r in range(2):
                 nc.sync.dma_start(gates[c, r][:], gate[r, c * P : (c + 1) * P, :])
 
-        slot_codes = [keep.tile([P, SLOTS], U32, name=f"slot_codes{g}", align_bytes=64) for g in range(PASSES)]
+        slot_codes = [keep.tile([P, SLOTS], U32, name="slot_codes0", align_bytes=64)]
         slot_scales = keep.tile([P, SLOTS], U8, name="slot_scales", align_bytes=64)
 
         def prepare_x(g, lo, on_vector):
@@ -89,64 +88,76 @@ def tile_routed_moe_kernel(tc, xT, w, b, gate, offs, pos1, pos2, out):
             )
 
         prepare_x(0, 0, HALF)
-        prepare_x(0, HALF, 160)
+        prepare_x(0, HALF, 0)
         nc.vector.tensor_copy(slot_codes[0][:], x_codes[0][:].bitcast(U32).indirect(offs_sb[:]))
         prepare_x(1, 0, 0)
         prepare_x(1, HALF, 0)
-        nc.vector.tensor_copy(slot_codes[1][:], x_codes[1][:].bitcast(U32).indirect(offs_sb[:]))
         nc.vector.tensor_copy(slot_scales[:], x_scales[:].indirect(offs_sb[:]))
 
-        y = [keep.tile([P, SLOTS], F32, name=f"y{c}") for c in range(BLOCKS)]
-        w_bf = keep.tile([P, BLOCKS, E, PASSES, P, PACK], BF16, name="w_bf", align_bytes=64)
-        w_codes = keep.tile([P, BLOCKS, E * PASSES, P], U32, name="w_codes", align_bytes=64)
-        w_scales = keep.tile([P, BLOCKS, E * PASSES, P], U8, name="w_scales", align_bytes=64)
         acc = {(e, c): psum.tile([P, C], F32, name=f"acc{e}{c}") for e in range(E) for c in range(BLOCKS)}
+        y = {}
 
-        def copy_both(copy, e, g):
-            copy(
-                w_bf[:, :, e, g, :, :].rearrange("p c (m i) t -> p c m t i", i=4),
-                w_raw[e, g][:].rearrange("p t (c m i) -> p c m t i", c=BLOCKS, i=4),
-            )
+        def staging(name, pieces, tag=None):
+            return keep.tile([P, pieces, P, PACK], BF16, name=name, tag=tag or name, align_bytes=64)
 
-        def copy_block(copy, e, g, c):
-            interleave(copy, w_bf[:, c, e, g, :, :], w_raw[e, g][:, :, c * P : (c + 1) * P])
+        def copy_both(copy, to, e, g):
+            copy(to.rearrange("p c (m i) t -> p c m t i", i=4), w_raw[e][:, g].rearrange("p t (c m i) -> p c m t i", c=BLOCKS, i=4))
 
-        def multiply(c, first, last):
+        def copy_block(copy, to, e, g, c):
+            interleave(copy, to, w_raw[e][:, g, :, c * P : (c + 1) * P])
+
+        def multiply(source, g, pairs):
+            name = f"{g}{pairs[0][0]}{pairs[0][1]}"
+            codes = keep.tile([P, len(pairs), P], U32, name="w_codes" + name, align_bytes=64)
+            scales = keep.tile([P, len(pairs), P], U8, name="w_scales" + name, align_bytes=64)
             nc.vector.quantize_mx(
-                out=w_codes[:, c, first:last, :].rearrange("p a n -> p (a n)").bitcast(FP8X4),
-                scales=w_scales[:, c, first:last, :].rearrange("p a n -> p (a n)"),
-                in_=w_bf[:, c].rearrange("p e g n t -> p (e g) (n t)")[:, first:last, :].rearrange("p a m -> p (a m)"),
+                out=codes[:].rearrange("p a n -> p (a n)").bitcast(FP8X4),
+                scales=scales[:].rearrange("p a n -> p (a n)"),
+                in_=source.rearrange("p a n t -> p (a n t)"),
             )
-            for piece in range(first, last):
-                e, g = divmod(piece, PASSES)
+            for j, (e, c) in enumerate(pairs):
                 slots = slice(e * C, (e + 1) * C)
                 nc.tensor.matmul_mx(
                     out=acc[e, c][:],
-                    lhsT=w_codes[:, c, piece, :].bitcast(FP8X4),
-                    lhsT_scale=w_scales[:, c, piece, :],
+                    lhsT=codes[:, j, :].bitcast(FP8X4),
+                    lhsT_scale=scales[:, j, :],
                     rhs=slot_codes[g][:, slots].bitcast(FP8X4),
                     rhs_scale=slot_scales[4 * g :, slots],
                     start=(g == 0),
                     stop=(g == PASSES - 1),
                 )
-                if g == PASSES - 1:
-                    nc.scalar.activation(y[c][:, slots], acc[e, c][:], SILU, bias=bias[:, c, e : e + 1])
 
-        for e, g in ((0, 0), (0, 1), (1, 0), (1, 1), (2, 0)):
-            copy_both(sc, e, g)
-        copy_block(sc, 2, 1, 0)
-        copy_block(sc, 3, 0, 0)
-        copy_block(ve, 3, 1, 0)
-        multiply(0, 0, 4)
-        multiply(0, 4, 6)
-        multiply(0, 6, 7)
-        multiply(0, 7, 8)
-        multiply(1, 0, 4)
-        copy_block(ve, 2, 1, 1)
-        multiply(1, 4, 6)
-        copy_block(ve, 3, 0, 1)
-        copy_block(sc, 3, 1, 1)
-        multiply(1, 6, 8)
+        def silu(e, c):
+            nc.scalar.activation(y[c][:, e * C : (e + 1) * C], acc[e, c][:], SILU, bias=bias[c][:, e : e + 1])
+
+        for pair in range(2):
+            bf = staging(f"w_bf0{pair}", 4)
+            for j in range(2):
+                e = 2 * pair + j
+                copy_both(ve if e == 0 else sc, bf[:, 2 * j : 2 * j + 2], e, 0)
+            multiply(bf[:], 0, [(2 * pair + j, c) for j in range(2) for c in range(BLOCKS)])
+        slot_codes.append(keep.tile([P, SLOTS], U32, name="slot_codes1", tag="w_bf01", align_bytes=64))
+        nc.vector.tensor_copy(slot_codes[1][:], x_codes[1][:].bitcast(U32).indirect(offs_sb[:]))
+
+        bf = staging("w_bf1", BLOCKS * E)
+        by_block = bf[:].rearrange("p (c e) n t -> p c e n t", c=BLOCKS)
+        for e in range(2):
+            copy_both(sc, by_block[:, :, e], e, 1)
+        for c in range(BLOCKS):
+            copy_block(sc, by_block[:, c, 2], 2, 1, c)
+        y[0] = keep.tile([P, SLOTS], F32, name="y0")
+        multiply(bf[:, 0:2], 1, [(0, 0), (1, 0)])
+        multiply(bf[:, 2:3], 1, [(2, 0)])
+        copy_block(ve, by_block[:, 0, 3], 3, 1, 0)
+        multiply(bf[:, 4:6], 1, [(0, 1), (1, 1)])
+        multiply(bf[:, 3:4], 1, [(3, 0)])
+        for e in range(E):
+            silu(e, 0)
+        copy_block(ve, by_block[:, 1, 3], 3, 1, 1)
+        multiply(bf[:, 6:8], 1, [(2, 1), (3, 1)])
+        y[1] = keep.tile([P, SLOTS], F32, name="y1", tag="bias0")
+        for e in range(E):
+            silu(e, 1)
 
         def gather(c, r, lo=0, hi=T):
             part = keep.tile([P, hi - lo], F32, name=f"part{c}{r}{lo}")

@@ -22,7 +22,6 @@ BLOCKS = N // P
 SLOTS = E * C
 HALF = T // 2
 WINDOW = 1376
-PE_COLS = 256
 
 
 def interleave(copy, out, in_):
@@ -149,12 +148,11 @@ def tile_routed_moe_kernel(tc, xT, w, b, gate, offs, pos1, pos2, out):
         multiply(bf[:, 0:2], 1, [(0, 0), (1, 0)])
         multiply(bf[:, 2:3], 1, [(2, 0)])
         copy_block(ve, by_block[:, 0, 3], 3, 1, 0)
-        multiply(bf[:, 4:6], 1, [(0, 1), (1, 1)])
+        copy_block(ve, by_block[:, 1, 3], 3, 1, 1)
         multiply(bf[:, 3:4], 1, [(3, 0)])
         for e in range(E):
             silu(e, 0)
-        copy_block(ve, by_block[:, 1, 3], 3, 1, 1)
-        multiply(bf[:, 6:8], 1, [(2, 1), (3, 1)])
+        multiply(bf[:, 4:8], 1, [(e, 1) for e in range(E)])
         y[1] = keep.tile([P, SLOTS], F32, name="y1", tag="bias0")
         for e in range(E):
             silu(e, 1)
@@ -164,17 +162,17 @@ def tile_routed_moe_kernel(tc, xT, w, b, gate, offs, pos1, pos2, out):
             nc.vector.tensor_tensor(part[:], y[c][:].indirect(pos_sb[r][:, lo // 16 : hi // 16]), gates[c, r][:, lo:hi], MULT)
             return part
 
-        total0_psum = psum.tile([P, PE_COLS], F32, name="acc00")
-        parts0 = []
+        banks = [psum.tile([P, HALF], F32, name=f"acc{h}0") for h in range(2)]
         for r in range(2):
-            parts0.append(gather(0, r))
-            nc.tensor.matmul(total0_psum[:], identity[:], parts0[r][:, :PE_COLS], start=(r == 0), stop=(r == 1))
-        total0 = keep.tile([P, T], F32, name="total0")
-        nc.scalar.copy(total0[:, :PE_COLS], total0_psum[:])
+            part = gather(0, r)
+            for h in range(2):
+                nc.tensor.matmul(banks[h][:], identity[:], part[:, h * HALF : (h + 1) * HALF], start=(r == 0), stop=(r == 1))
+        for h in range(2):
+            total0 = keep.tile([P, HALF], F32, name=f"total0{h}")
+            nc.scalar.copy(total0[:], banks[h][:])
+            nc.scalar.dma_start(out[:P, h * HALF : (h + 1) * HALF], total0[:])
 
         first = gather(1, 0)
-        nc.vector.tensor_tensor(total0[:, PE_COLS:], parts0[0][:, PE_COLS:], parts0[1][:, PE_COLS:], ADD)
-        nc.sync.dma_start(out[:P, :], total0[:])
         seconds = [gather(1, 1, lo, lo + HALF) for lo in (0, HALF)]
         for i, lo in enumerate((0, HALF)):
             total1 = keep.tile([P, HALF], F32, name=f"total1{i}")

@@ -61,15 +61,17 @@ def tile_routed_moe_kernel(tc, xT, w, b, gate, offs, pos1, pos2, out):
         nc.sync.dma_start(offs_sb[:], offs)
         nc.sync.dma_start(x_raw[1][:], rows(xT, 1))
         for g in range(PASSES):
-            for e in range(E):
+            for e in range(E - g):
                 nc.sync.dma_start(w_raw[e][:, g], rows(w[e], g))
+        nc.sync.dma_start(w_raw[3][:, 1, :, :P], rows(w[3], 1)[:, :, :P])
         nc.sync.dma_start(bias[0][:], b[:P, :])
-        nc.sync.dma_start(pos_sb[0][:], pos1)
+        nc.sync.dma_start(w_raw[3][:, 1, :, P:], rows(w[3], 1)[:, :, P:])
+        for r, pos in enumerate((pos1, pos2)):
+            nc.sync.dma_start(pos_sb[r][:], pos)
+            nc.sync.dma_start(gates[0, r][:], gate[r, :P, :])
         nc.sync.dma_start(bias[1][:], b[P:, :])
-        nc.sync.dma_start(pos_sb[1][:], pos2)
-        for c in range(BLOCKS):
-            for r in range(2):
-                nc.sync.dma_start(gates[c, r][:], gate[r, c * P : (c + 1) * P, :])
+        for r in range(2):
+            nc.sync.dma_start(gates[1, r][:], gate[r, P:, :])
 
         slot_codes = [keep.tile([P, SLOTS], U32, name="slot_codes0", align_bytes=64)]
         slot_scales = keep.tile([P, SLOTS], U8, name="slot_scales", align_bytes=64)

@@ -39,7 +39,7 @@ def tile_routed_moe_kernel(tc, xT, w, b, gate, offs, pos1, pos2, out):
         offs_sb = lists.tile([P, SLOTS // 16], U16, name="offs_sb")
         pos_sb = [lists.tile([P, T // 16], U16, name=f"pos_sb{r}") for r in range(2)]
         x_raw = [keep.tile([P, PACK, T], F32, name=f"x_raw{g}") for g in range(PASSES)]
-        w_raw = [keep.tile([P, PASSES, PACK, N], F32, name=f"w_raw{e}") for e in range(E)]
+        w_raw = {(e, g): keep.tile([P, PACK, N], F32, name=f"w_raw{e}{g}", align_bytes=64) for e in range(E) for g in range(PASSES)}
         bias = [keep.tile([P, E], F32, name=f"bias{c}") for c in range(BLOCKS)]
         gates = {(c, r): keep.tile([P, T], F32, name=f"gates{c}{r}") for c in range(BLOCKS) for r in range(2)}
         x_scales = keep.tile([P, WINDOW], U8, name="x_scales", align_bytes=64)
@@ -62,10 +62,10 @@ def tile_routed_moe_kernel(tc, xT, w, b, gate, offs, pos1, pos2, out):
         nc.sync.dma_start(x_raw[1][:], rows(xT, 1))
         for g in range(PASSES):
             for e in range(E - g):
-                nc.sync.dma_start(w_raw[e][:, g], rows(w[e], g))
-        nc.sync.dma_start(w_raw[3][:, 1, :, :P], rows(w[3], 1)[:, :, :P])
+                nc.sync.dma_start(w_raw[e, g][:], rows(w[e], g))
+        nc.sync.dma_start(w_raw[3, 1][:, :, :P], rows(w[3], 1)[:, :, :P])
         nc.sync.dma_start(bias[0][:], b[:P, :])
-        nc.sync.dma_start(w_raw[3][:, 1, :, P:], rows(w[3], 1)[:, :, P:])
+        nc.sync.dma_start(w_raw[3, 1][:, :, P:], rows(w[3], 1)[:, :, P:])
         for r, pos in enumerate((pos1, pos2)):
             nc.sync.dma_start(pos_sb[r][:], pos)
             nc.sync.dma_start(gates[0, r][:], gate[r, :P, :])
@@ -102,14 +102,14 @@ def tile_routed_moe_kernel(tc, xT, w, b, gate, offs, pos1, pos2, out):
             return keep.tile([P, pieces, P, PACK], BF16, name=name, tag=tag or name, align_bytes=64)
 
         def copy_both(copy, to, e, g):
-            copy(to.rearrange("p c (m i) t -> p c m t i", i=4), w_raw[e][:, g].rearrange("p t (c m i) -> p c m t i", c=BLOCKS, i=4))
+            copy(to.rearrange("p c (m i) t -> p c m t i", i=4), w_raw[e, g][:].rearrange("p t (c m i) -> p c m t i", c=BLOCKS, i=4))
 
         def copy_block(copy, to, e, g, c):
-            interleave(copy, to, w_raw[e][:, g, :, c * P : (c + 1) * P])
+            interleave(copy, to, w_raw[e, g][:, :, c * P : (c + 1) * P])
 
-        def multiply(source, g, pairs):
+        def multiply(source, g, pairs, after=None):
             name = f"{g}{pairs[0][0]}{pairs[0][1]}"
-            codes = keep.tile([P, len(pairs), P], U32, name="w_codes" + name, align_bytes=64)
+            codes = keep.tile([P, len(pairs), P], U32, name="w_codes" + name, tag=after or "w_codes" + name, align_bytes=64)
             scales = keep.tile([P, len(pairs), P], U8, name="w_scales" + name, align_bytes=64)
             nc.vector.quantize_mx(
                 out=codes[:].rearrange("p a n -> p (a n)").bitcast(FP8X4),
@@ -131,13 +131,13 @@ def tile_routed_moe_kernel(tc, xT, w, b, gate, offs, pos1, pos2, out):
         def silu(e, c):
             nc.scalar.activation(y[c][:, e * C : (e + 1) * C], acc[e, c][:], SILU, bias=bias[c][:, e : e + 1])
 
-        for pair in range(2):
-            bf = staging(f"w_bf0{pair}", 4)
-            for j in range(2):
-                e = 2 * pair + j
-                copy_both(ve if e == 0 else sc, bf[:, 2 * j : 2 * j + 2], e, 0)
-            multiply(bf[:], 0, [(2 * pair + j, c) for j in range(2) for c in range(BLOCKS)])
-        slot_codes.append(keep.tile([P, SLOTS], U32, name="slot_codes1", tag="w_bf01", align_bytes=64))
+        zero = [staging(f"w_bf0{c}", E) for c in range(BLOCKS)]
+        for e in range(E):
+            for c in range(BLOCKS):
+                copy_block(ve if e == 0 else sc, zero[c][:, e], e, 0, c)
+        multiply(zero[0][:], 0, [(e, 0) for e in range(E)])
+        multiply(zero[1][:, 0:2], 0, [(0, 1), (1, 1)], after="w_raw20")
+        slot_codes.append(keep.tile([P, SLOTS], U32, name="slot_codes1", tag="w_bf00", align_bytes=64))
         nc.vector.tensor_copy(slot_codes[1][:], x_codes[1][:].bitcast(U32).indirect(offs_sb[:]))
 
         bf = staging("w_bf1", BLOCKS * E)
@@ -154,6 +154,7 @@ def tile_routed_moe_kernel(tc, xT, w, b, gate, offs, pos1, pos2, out):
         multiply(bf[:, 3:4], 1, [(3, 0)])
         for e in range(E):
             silu(e, 0)
+        multiply(zero[1][:, 2:4], 0, [(2, 1), (3, 1)], after="w_raw31")
         multiply(bf[:, 4:8], 1, [(e, 1) for e in range(E)])
         y[1] = keep.tile([P, SLOTS], F32, name="y1", tag="bias0")
         for e in range(E):

@@ -22,6 +22,8 @@ BLOCKS = N // P
 SLOTS = E * C
 HALF = T // 2
 WINDOW = 1376
+FIRST_SHARE = 64
+SECOND_SHARE = 160
 
 
 def interleave(copy, out, in_):
@@ -33,6 +35,7 @@ def tile_routed_moe_kernel(tc, xT, w, b, gate, offs, pos1, pos2, out):
     with (
         tc.tile_pool(name="lists", bufs=1) as lists,
         tc.tile_pool(name="keep", bufs=1) as keep,
+        tc.tile_pool(name="turns", bufs=1) as turns,
         tc.psum_pool(name="psum", bufs=1) as psum,
     ):
         sc, ve = nc.scalar.copy, nc.vector.tensor_copy
@@ -76,23 +79,28 @@ def tile_routed_moe_kernel(tc, xT, w, b, gate, offs, pos1, pos2, out):
         slot_codes = [keep.tile([P, SLOTS], U32, name="slot_codes0", align_bytes=64)]
         slot_scales = keep.tile([P, SLOTS], U8, name="slot_scales", align_bytes=64)
 
-        def prepare_x(g, lo, on_vector):
+        def copy_x(g, lo, on_vector):
             x_bf = keep.tile([P, HALF, PACK], BF16, name=f"x_bf{g}{lo}", align_bytes=64)
             if on_vector > 0:
                 interleave(ve, x_bf[:, :on_vector, :], x_raw[g][:, :, lo : lo + on_vector])
             if on_vector < HALF:
                 interleave(sc, x_bf[:, on_vector:, :], x_raw[g][:, :, lo + on_vector : lo + HALF])
+            return x_bf
+
+        def quantize_x(g, lo, x_bf):
             nc.vector.quantize_mx(
                 out=x_codes[g][:, lo : lo + HALF].bitcast(FP8X4),
                 scales=x_scales[4 * g :, lo : lo + HALF],
                 in_=x_bf[:].rearrange("p n t -> p (n t)"),
             )
 
-        prepare_x(0, 0, HALF)
-        prepare_x(0, HALF, 0)
+        halves = [copy_x(0, 0, HALF), copy_x(0, HALF, FIRST_SHARE)]
+        for h in range(2):
+            quantize_x(0, h * HALF, halves[h])
         nc.vector.tensor_copy(slot_codes[0][:], x_codes[0][:].bitcast(U32).indirect(offs_sb[:]))
-        prepare_x(1, 0, 0)
-        prepare_x(1, HALF, 0)
+        halves = [copy_x(1, 0, 0), copy_x(1, HALF, SECOND_SHARE)]
+        for h in range(2):
+            quantize_x(1, h * HALF, halves[h])
         nc.vector.tensor_copy(slot_scales[:], x_scales[:].indirect(offs_sb[:]))
 
         acc = {(e, c): psum.tile([P, C], F32, name=f"acc{e}{c}") for e in range(E) for c in range(BLOCKS)}
@@ -107,8 +115,8 @@ def tile_routed_moe_kernel(tc, xT, w, b, gate, offs, pos1, pos2, out):
         def copy_block(copy, to, e, g, c):
             interleave(copy, to, w_raw[e, g][:, :, c * P : (c + 1) * P])
 
-        def multiply(source, g, pairs, after=None):
-            name = f"{g}{pairs[0][0]}{pairs[0][1]}"
+        def multiply(source, pairs, after=None):
+            name = "%d%d%d" % pairs[0]
             codes = keep.tile([P, len(pairs), P], U32, name="w_codes" + name, tag=after or "w_codes" + name, align_bytes=64)
             scales = keep.tile([P, len(pairs), P], U8, name="w_scales" + name, align_bytes=64)
             nc.vector.quantize_mx(
@@ -116,7 +124,7 @@ def tile_routed_moe_kernel(tc, xT, w, b, gate, offs, pos1, pos2, out):
                 scales=scales[:].rearrange("p a n -> p (a n)"),
                 in_=source.rearrange("p a n t -> p (a n t)"),
             )
-            for j, (e, c) in enumerate(pairs):
+            for j, (e, g, c) in enumerate(pairs):
                 slots = slice(e * C, (e + 1) * C)
                 nc.tensor.matmul_mx(
                     out=acc[e, c][:],
@@ -131,31 +139,42 @@ def tile_routed_moe_kernel(tc, xT, w, b, gate, offs, pos1, pos2, out):
         def silu(e, c):
             nc.scalar.activation(y[c][:, e * C : (e + 1) * C], acc[e, c][:], SILU, bias=bias[c][:, e : e + 1])
 
-        zero = [staging(f"w_bf0{c}", E) for c in range(BLOCKS)]
-        for e in range(E):
-            for c in range(BLOCKS):
-                copy_block(ve if e == 0 else sc, zero[c][:, e], e, 0, c)
-        multiply(zero[0][:], 0, [(e, 0) for e in range(E)])
-        multiply(zero[1][:, 0:2], 0, [(0, 1), (1, 1)], after="w_raw20")
-        slot_codes.append(keep.tile([P, SLOTS], U32, name="slot_codes1", tag="w_bf00", align_bytes=64))
-        nc.vector.tensor_copy(slot_codes[1][:], x_codes[1][:].bitcast(U32).indirect(offs_sb[:]))
+        def gp(to, source):
+            nc.gpsimd.tensor_scalar(to, source, 1.0, 0.0, MULT, ADD)
 
+        block0 = turns.tile([P, E, P, PACK], BF16, name="block0", offset=1984, align_bytes=64)
+        early = staging("w_early", 2, tag=f"x_bf1{HALF}")
         bf = staging("w_bf1", BLOCKS * E)
+        copy_block(sc, block0[:, 0], 0, 0, 0)
+        copy_block(gp, early[:, 0], 0, 0, 1)
+        copy_block(sc, block0[:, 1], 1, 0, 0)
+        copy_block(sc, early[:, 1], 1, 0, 1)
+        copy_block(sc, block0[:, 2], 2, 0, 0)
+        copy_block(sc, block0[:, 3], 3, 0, 0)
+        copy_block(sc, bf[:, 4], 3, 0, 1)
+        multiply(block0[:], [(e, 0, 0) for e in range(E)])
+        multiply(early[:], [(0, 0, 1), (1, 0, 1)])
+        slot_codes.append(turns.tile([P, SLOTS], U32, name="slot_codes1", offset=2048, align_bytes=64))
+        nc.vector.tensor_copy(slot_codes[1][:], x_codes[1][:].bitcast(U32).indirect(offs_sb[:]))
+        late = turns.tile([P, 2, P, PACK], BF16, name="w_late", offset=0, align_bytes=64)
+        copy_block(gp, late[:, 0], 2, 0, 1)
+
+        copy_block(sc, bf[:, 0], 0, 1, 0)
+        copy_block(sc, late[:, 1], 0, 1, 1)
         by_block = bf[:].rearrange("p (c e) n t -> p c e n t", c=BLOCKS)
-        for e in range(2):
-            copy_both(sc, by_block[:, :, e], e, 1)
+        copy_both(sc, by_block[:, :, 1], 1, 1)
         for c in range(BLOCKS):
             copy_block(sc, by_block[:, c, 2], 2, 1, c)
         y[0] = keep.tile([P, SLOTS], F32, name="y0")
-        multiply(bf[:, 0:2], 1, [(0, 0), (1, 0)])
-        multiply(bf[:, 2:3], 1, [(2, 0)])
+        multiply(bf[:, 0:2], [(0, 1, 0), (1, 1, 0)])
+        multiply(bf[:, 2:3], [(2, 1, 0)])
         copy_block(ve, by_block[:, 0, 3], 3, 1, 0)
         copy_block(ve, by_block[:, 1, 3], 3, 1, 1)
-        multiply(bf[:, 3:4], 1, [(3, 0)])
+        multiply(bf[:, 3:4], [(3, 1, 0)])
         for e in range(E):
             silu(e, 0)
-        multiply(zero[1][:, 2:4], 0, [(2, 1), (3, 1)], after="w_raw31")
-        multiply(bf[:, 4:8], 1, [(e, 1) for e in range(E)])
+        multiply(late[:], [(2, 0, 1), (0, 1, 1)], after="w_raw31")
+        multiply(bf[:, 4:8], [(3, 0, 1), (1, 1, 1), (2, 1, 1), (3, 1, 1)])
         y[1] = keep.tile([P, SLOTS], F32, name="y1", tag="bias0")
         for e in range(E):
             silu(e, 1)

@@ -42,7 +42,8 @@ def tile_routed_moe_kernel(tc, xT, w, b, gate, offs, pos1, pos2, out):
         offs_sb = lists.tile([P, SLOTS // 16], U16, name="offs_sb")
         pos_sb = [lists.tile([P, T // 16], U16, name=f"pos_sb{r}") for r in range(2)]
         x_raw = [keep.tile([P, PACK, T], F32, name=f"x_raw{g}") for g in range(PASSES)]
-        w_raw = {(e, g): keep.tile([P, PACK, N], F32, name=f"w_raw{e}{g}", align_bytes=64) for e in range(E) for g in range(PASSES)}
+        w_raw = {(e, g): keep.tile([P, PACK, N], F32, name=f"w_raw{e}{g}", align_bytes=64) for g in range(PASSES) for e in range(E - g)}
+        w_last = [keep.tile([P, PACK, P], F32, name=f"w_last{c}", align_bytes=64) for c in range(BLOCKS)]
         bias = [keep.tile([P, E], F32, name=f"bias{c}") for c in range(BLOCKS)]
         gates = {(c, r): keep.tile([P, T], F32, name=f"gates{c}{r}") for c in range(BLOCKS) for r in range(2)}
         x_scales = keep.tile([P, WINDOW], U8, name="x_scales", align_bytes=64)
@@ -66,9 +67,9 @@ def tile_routed_moe_kernel(tc, xT, w, b, gate, offs, pos1, pos2, out):
         for g in range(PASSES):
             for e in range(E - g):
                 nc.sync.dma_start(w_raw[e, g][:], rows(w[e], g))
-        nc.sync.dma_start(w_raw[3, 1][:, :, :P], rows(w[3], 1)[:, :, :P])
+        nc.sync.dma_start(w_last[0][:], rows(w[3], 1)[:, :, :P])
         nc.sync.dma_start(bias[0][:], b[:P, :])
-        nc.sync.dma_start(w_raw[3, 1][:, :, P:], rows(w[3], 1)[:, :, P:])
+        nc.sync.dma_start(w_last[1][:], rows(w[3], 1)[:, :, P:])
         for r, pos in enumerate((pos1, pos2)):
             nc.sync.dma_start(pos_sb[r][:], pos)
             nc.sync.dma_start(gates[0, r][:], gate[r, :P, :])
@@ -94,6 +95,50 @@ def tile_routed_moe_kernel(tc, xT, w, b, gate, offs, pos1, pos2, out):
                 in_=x_bf[:].rearrange("p n t -> p (n t)"),
             )
 
+        acc = {(e, c): psum.tile([P, C], F32, name=f"acc{e}{c}") for e in range(E) for c in range(BLOCKS)}
+        y = {}
+        w_mx = {}
+
+        def staging(name, pieces, tag=None, offset=None):
+            if offset is not None:
+                return turns.tile([P, pieces, P, PACK], BF16, name=name, offset=offset, align_bytes=64)
+            return keep.tile([P, pieces, P, PACK], BF16, name=name, tag=tag or name, align_bytes=64)
+
+        def copy_block(copy, to, e, g, c):
+            source = w_last[c][:] if (e, g) == (3, 1) else w_raw[e, g][:, :, c * P : (c + 1) * P]
+            interleave(copy, to, source)
+
+        def quantize_w(source, pieces, after=None):
+            name = "%d%d%d" % pieces[0]
+            codes = keep.tile([P, len(pieces), P], U32, name="w_codes" + name, tag=after or "w_codes" + name, align_bytes=64)
+            scales = keep.tile([P, len(pieces), P], U8, name="w_scales" + name, align_bytes=64)
+            nc.vector.quantize_mx(
+                out=codes[:].rearrange("p a n -> p (a n)").bitcast(FP8X4),
+                scales=scales[:].rearrange("p a n -> p (a n)"),
+                in_=source[:].rearrange("p a n t -> p (a n t)"),
+            )
+            for j, piece in enumerate(pieces):
+                w_mx[piece] = (codes[:, j, :], scales[:, j, :])
+
+        def multiply(e, g, c):
+            slots = slice(e * C, (e + 1) * C)
+            codes, scales = w_mx[e, g, c]
+            nc.tensor.matmul_mx(
+                out=acc[e, c][:],
+                lhsT=codes.bitcast(FP8X4),
+                lhsT_scale=scales,
+                rhs=slot_codes[g][:, slots].bitcast(FP8X4),
+                rhs_scale=slot_scales[4 * g :, slots],
+                start=(g == 0),
+                stop=(g == PASSES - 1),
+            )
+
+        def silu(e, c):
+            nc.scalar.activation(y[c][:, e * C : (e + 1) * C], acc[e, c][:], SILU, bias=bias[c][:, e : e + 1])
+
+        def gp(to, source):
+            nc.gpsimd.tensor_scalar(to, source, 1.0, 0.0, MULT, ADD)
+
         halves = [copy_x(0, 0, HALF), copy_x(0, HALF, FIRST_SHARE)]
         for h in range(2):
             quantize_x(0, h * HALF, halves[h])
@@ -103,80 +148,55 @@ def tile_routed_moe_kernel(tc, xT, w, b, gate, offs, pos1, pos2, out):
             quantize_x(1, h * HALF, halves[h])
         nc.vector.tensor_copy(slot_scales[:], x_scales[:].indirect(offs_sb[:]))
 
-        acc = {(e, c): psum.tile([P, C], F32, name=f"acc{e}{c}") for e in range(E) for c in range(BLOCKS)}
-        y = {}
-
-        def staging(name, pieces, tag=None):
-            return keep.tile([P, pieces, P, PACK], BF16, name=name, tag=tag or name, align_bytes=64)
-
-        def copy_both(copy, to, e, g):
-            copy(to.rearrange("p c (m i) t -> p c m t i", i=4), w_raw[e, g][:].rearrange("p t (c m i) -> p c m t i", c=BLOCKS, i=4))
-
-        def copy_block(copy, to, e, g, c):
-            interleave(copy, to, w_raw[e, g][:, :, c * P : (c + 1) * P])
-
-        def multiply(source, pairs, after=None):
-            name = "%d%d%d" % pairs[0]
-            codes = keep.tile([P, len(pairs), P], U32, name="w_codes" + name, tag=after or "w_codes" + name, align_bytes=64)
-            scales = keep.tile([P, len(pairs), P], U8, name="w_scales" + name, align_bytes=64)
-            nc.vector.quantize_mx(
-                out=codes[:].rearrange("p a n -> p (a n)").bitcast(FP8X4),
-                scales=scales[:].rearrange("p a n -> p (a n)"),
-                in_=source.rearrange("p a n t -> p (a n t)"),
-            )
-            for j, (e, g, c) in enumerate(pairs):
-                slots = slice(e * C, (e + 1) * C)
-                nc.tensor.matmul_mx(
-                    out=acc[e, c][:],
-                    lhsT=codes[:, j, :].bitcast(FP8X4),
-                    lhsT_scale=scales[:, j, :],
-                    rhs=slot_codes[g][:, slots].bitcast(FP8X4),
-                    rhs_scale=slot_scales[4 * g :, slots],
-                    start=(g == 0),
-                    stop=(g == PASSES - 1),
-                )
-
-        def silu(e, c):
-            nc.scalar.activation(y[c][:, e * C : (e + 1) * C], acc[e, c][:], SILU, bias=bias[c][:, e : e + 1])
-
-        def gp(to, source):
-            nc.gpsimd.tensor_scalar(to, source, 1.0, 0.0, MULT, ADD)
-
-        block0 = turns.tile([P, E, P, PACK], BF16, name="block0", offset=1984, align_bytes=64)
-        early = staging("w_early", 2, tag=f"x_bf1{HALF}")
-        bf = staging("w_bf1", BLOCKS * E)
-        copy_block(sc, block0[:, 0], 0, 0, 0)
-        copy_block(gp, early[:, 0], 0, 0, 1)
-        copy_block(sc, block0[:, 1], 1, 0, 0)
-        copy_block(sc, early[:, 1], 1, 0, 1)
-        copy_block(sc, block0[:, 2], 2, 0, 0)
-        copy_block(sc, block0[:, 3], 3, 0, 0)
-        copy_block(sc, bf[:, 4], 3, 0, 1)
-        multiply(block0[:], [(e, 0, 0) for e in range(E)])
-        multiply(early[:], [(0, 0, 1), (1, 0, 1)])
-        slot_codes.append(turns.tile([P, SLOTS], U32, name="slot_codes1", offset=2048, align_bytes=64))
+        by_gpsimd = staging("by_gpsimd", 2, tag=f"x_bf1{HALF}")
+        low = staging("low", 2, offset=64)
+        high = staging("high", 2, offset=2112)
+        by_scalar = staging("by_scalar", 2)
+        copy_block(gp, by_gpsimd[:, 0], 0, 0, 1)
+        copy_block(gp, by_gpsimd[:, 1], 2, 0, 1)
+        copy_block(sc, low[:, 0], 0, 0, 0)
+        copy_block(sc, low[:, 1], 1, 0, 0)
+        copy_block(sc, by_scalar[:, 0], 1, 0, 1)
+        copy_block(sc, high[:, 0], 2, 0, 0)
+        copy_block(sc, high[:, 1], 3, 0, 0)
+        copy_block(sc, by_scalar[:, 1], 3, 0, 1)
+        quantize_w(high, [(2, 0, 0), (3, 0, 0)])
+        quantize_w(low, [(0, 0, 0), (1, 0, 0)], after="x_scales")
+        for e in (2, 3, 0, 1):
+            multiply(e, 0, 0)
+        slot_codes.append(turns.tile([P, SLOTS], U32, name="slot_codes1", offset=4096, align_bytes=64))
         nc.vector.tensor_copy(slot_codes[1][:], x_codes[1][:].bitcast(U32).indirect(offs_sb[:]))
-        late = turns.tile([P, 2, P, PACK], BF16, name="w_late", offset=0, align_bytes=64)
-        copy_block(gp, late[:, 0], 2, 0, 1)
 
-        copy_block(sc, bf[:, 0], 0, 1, 0)
-        copy_block(sc, late[:, 1], 0, 1, 1)
-        by_block = bf[:].rearrange("p (c e) n t -> p c e n t", c=BLOCKS)
-        copy_both(sc, by_block[:, :, 1], 1, 1)
-        for c in range(BLOCKS):
-            copy_block(sc, by_block[:, c, 2], 2, 1, c)
+        mixed = staging("mixed", 2, offset=1024)
+        copy_block(gp, mixed[:, 0], 0, 1, 1)
+        second = staging("second", 2)
+        s210 = staging("s210", 1)
+        s211 = staging("s211", 1)
+        copy_block(sc, second[:, 0], 0, 1, 0)
+        copy_block(sc, second[:, 1], 1, 1, 0)
+        copy_block(sc, mixed[:, 1], 1, 1, 1)
+        copy_block(sc, s210[:, 0], 2, 1, 0)
+        copy_block(sc, s211[:, 0], 2, 1, 1)
+        quantize_w(second, [(0, 1, 0), (1, 1, 0)])
+        quantize_w(mixed, [(0, 1, 1), (1, 1, 1)], after="x_codes1")
+        quantize_w(s210, [(2, 1, 0)])
+        s310 = staging("s310", 1)
+        copy_block(ve, s310[:, 0], 3, 1, 0)
+        quantize_w(by_gpsimd, [(0, 0, 1), (2, 0, 1)], after="s210")
+        quantize_w(s310, [(3, 1, 0)])
         y[0] = keep.tile([P, SLOTS], F32, name="y0")
-        multiply(bf[:, 0:2], [(0, 1, 0), (1, 1, 0)])
-        multiply(bf[:, 2:3], [(2, 1, 0)])
-        copy_block(ve, by_block[:, 0, 3], 3, 1, 0)
-        copy_block(ve, by_block[:, 1, 3], 3, 1, 1)
-        multiply(bf[:, 3:4], [(3, 1, 0)])
         for e in range(E):
+            multiply(e, 1, 0)
             silu(e, 0)
-        multiply(late[:], [(2, 0, 1), (0, 1, 1)], after="w_raw31")
-        multiply(bf[:, 4:8], [(3, 0, 1), (1, 1, 1), (2, 1, 1), (3, 1, 1)])
+        quantize_w(by_scalar, [(1, 0, 1), (3, 0, 1)], after="w_last0")
+        s311 = staging("s311", 1, tag="s310")
+        copy_block(ve, s311[:, 0], 3, 1, 1)
+        quantize_w(s211, [(2, 1, 1)], after="by_scalar")
+        quantize_w(s311, [(3, 1, 1)])
         y[1] = keep.tile([P, SLOTS], F32, name="y1", tag="bias0")
         for e in range(E):
+            for g in range(PASSES):
+                multiply(e, g, 1)
             silu(e, 1)
 
         def gather(c, r, lo=0, hi=T):

@@ -148,55 +148,52 @@ def tile_routed_moe_kernel(tc, xT, w, b, gate, offs, pos1, pos2, out):
             quantize_x(1, h * HALF, halves[h])
         nc.vector.tensor_copy(slot_scales[:], x_scales[:].indirect(offs_sb[:]))
 
-        by_gpsimd = staging("by_gpsimd", 2, tag=f"x_bf1{HALF}")
-        low = staging("low", 2, offset=64)
-        high = staging("high", 2, offset=2112)
-        by_scalar = staging("by_scalar", 2)
-        copy_block(gp, by_gpsimd[:, 0], 0, 0, 1)
-        copy_block(gp, by_gpsimd[:, 1], 2, 0, 1)
+        late0 = staging("late0", E, tag=f"x_bf1{HALF}")
+        low = staging("low", 2, offset=2048)
+        high = staging("high", 2)
+        copy_block(gp, late0[:, 0], 0, 0, 1)
         copy_block(sc, low[:, 0], 0, 0, 0)
         copy_block(sc, low[:, 1], 1, 0, 0)
-        copy_block(sc, by_scalar[:, 0], 1, 0, 1)
+        copy_block(sc, late0[:, 1], 1, 0, 1)
         copy_block(sc, high[:, 0], 2, 0, 0)
         copy_block(sc, high[:, 1], 3, 0, 0)
-        copy_block(sc, by_scalar[:, 1], 3, 0, 1)
+        copy_block(sc, late0[:, 2], 2, 0, 1)
+        copy_block(sc, late0[:, 3], 3, 0, 1)
+        quantize_w(low, [(0, 0, 0), (1, 0, 0)])
         quantize_w(high, [(2, 0, 0), (3, 0, 0)])
-        quantize_w(low, [(0, 0, 0), (1, 0, 0)], after="x_scales")
-        for e in (2, 3, 0, 1):
+        for e in range(E):
             multiply(e, 0, 0)
-        slot_codes.append(turns.tile([P, SLOTS], U32, name="slot_codes1", offset=4096, align_bytes=64))
+        slot_codes.append(turns.tile([P, SLOTS], U32, name="slot_codes1", offset=4032, align_bytes=64))
         nc.vector.tensor_copy(slot_codes[1][:], x_codes[1][:].bitcast(U32).indirect(offs_sb[:]))
 
-        mixed = staging("mixed", 2, offset=1024)
-        copy_block(gp, mixed[:, 0], 0, 1, 1)
+        late1 = staging("late1", 2, offset=1024)
+        copy_block(gp, late1[:, 0], 0, 1, 1)
         second = staging("second", 2)
         s210 = staging("s210", 1)
-        s211 = staging("s211", 1)
+        last = staging("last", 2)
         copy_block(sc, second[:, 0], 0, 1, 0)
         copy_block(sc, second[:, 1], 1, 1, 0)
-        copy_block(sc, mixed[:, 1], 1, 1, 1)
+        copy_block(sc, late1[:, 1], 1, 1, 1)
         copy_block(sc, s210[:, 0], 2, 1, 0)
-        copy_block(sc, s211[:, 0], 2, 1, 1)
+        copy_block(sc, last[:, 0], 2, 1, 1)
         quantize_w(second, [(0, 1, 0), (1, 1, 0)])
-        quantize_w(mixed, [(0, 1, 1), (1, 1, 1)], after="x_codes1")
-        quantize_w(s210, [(2, 1, 0)])
         s310 = staging("s310", 1)
         copy_block(ve, s310[:, 0], 3, 1, 0)
-        quantize_w(by_gpsimd, [(0, 0, 1), (2, 0, 1)], after="s210")
+        quantize_w(s210, [(2, 1, 0)])
         quantize_w(s310, [(3, 1, 0)])
         y[0] = keep.tile([P, SLOTS], F32, name="y0")
         for e in range(E):
             multiply(e, 1, 0)
             silu(e, 0)
-        quantize_w(by_scalar, [(1, 0, 1), (3, 0, 1)], after="w_last0")
-        s311 = staging("s311", 1, tag="s310")
-        copy_block(ve, s311[:, 0], 3, 1, 1)
-        quantize_w(s211, [(2, 1, 1)], after="by_scalar")
-        quantize_w(s311, [(3, 1, 1)])
+        quantize_w(late0, [(e, 0, 1) for e in range(E)], after="w_last0")
+        copy_block(ve, last[:, 1], 3, 1, 1)
+        quantize_w(late1, [(0, 1, 1), (1, 1, 1)], after="s310")
+        quantize_w(last, [(2, 1, 1), (3, 1, 1)])
         y[1] = keep.tile([P, SLOTS], F32, name="y1", tag="bias0")
-        for e in range(E):
-            for g in range(PASSES):
+        for g in range(PASSES):
+            for e in range(E):
                 multiply(e, g, 1)
+        for e in range(E):
             silu(e, 1)
 
         def gather(c, r, lo=0, hi=T):

@@ -13,6 +13,7 @@ U8 = mybir.dt.uint8
 FP8X4 = mybir.dt.float8_e4m3fn_x4
 MULT, ADD = mybir.AluOpType.mult, mybir.AluOpType.add
 SILU = mybir.ActivationFunctionType.Silu
+COPY = mybir.ActivationFunctionType.Copy
 
 P = 128
 PACK = 4
@@ -206,13 +207,27 @@ def tile_routed_moe_kernel(tc, xT, w, b, gate, offs, pos1, pos2, out):
             part = gather(0, r)
             for h in range(2):
                 nc.tensor.matmul(banks[h][:], identity[:], part[:, h * HALF : (h + 1) * HALF], start=(r == 0), stop=(r == 1))
-        for h in range(2):
-            total0 = keep.tile([P, HALF], F32, name=f"total0{h}")
-            nc.scalar.copy(total0[:], banks[h][:])
-            nc.scalar.dma_start(out[:P, h * HALF : (h + 1) * HALF], total0[:])
 
-        first = gather(1, 0)
-        seconds = [gather(1, 1, lo, lo + HALF) for lo in (0, HALF)]
+        def fetch(c, r, lo, hi):
+            plain = keep.tile([P, hi - lo], F32, name=f"plain{c}{r}{lo}")
+            nc.scalar.activation(plain[:], y[c][:].indirect(pos_sb[r][:, lo // 16 : hi // 16]), COPY)
+            return plain
+
+        def times_gate(plain, c, r, lo, hi):
+            part = keep.tile([P, hi - lo], F32, name=f"part{c}{r}{lo}")
+            nc.vector.tensor_tensor(part[:], plain[:], gates[c, r][:, lo:hi], MULT)
+            return part
+
+        plain_first = fetch(1, 0, 0, T)
+        plain_second = fetch(1, 1, HALF, T)
+        seconds = [gather(1, 1, 0, HALF)]
+        first = times_gate(plain_first, 1, 0, 0, T)
+        seconds.append(times_gate(plain_second, 1, 1, HALF, T))
+        total0 = keep.tile([P, T], F32, name="total0", tag="bias0")
+        for h in range(2):
+            columns = slice(h * HALF, (h + 1) * HALF)
+            nc.scalar.copy(total0[:, columns], banks[h][:])
+            nc.scalar.dma_start(out[:P, columns], total0[:, columns])
         for i, lo in enumerate((0, HALF)):
             total1 = keep.tile([P, HALF], F32, name=f"total1{i}")
             nc.vector.tensor_tensor(total1[:], first[:, lo : lo + HALF], seconds[i][:], ADD)

@@ -149,7 +149,8 @@ def tile_routed_moe_kernel(tc, xT, w, b, gate, offs, pos1, pos2, out):
             quantize_x(1, h * HALF, halves[h])
         nc.vector.tensor_copy(slot_scales[:], x_scales[:].indirect(offs_sb[:]))
 
-        late0 = staging("late0", E, tag=f"x_bf1{HALF}")
+        late0 = staging("late0", 2, tag=f"x_bf1{HALF}")
+        late0b = staging("late0b", 2)
         low = staging("low", 2, offset=2048)
         high = staging("high", 2)
         copy_block(gp, late0[:, 0], 0, 0, 1)
@@ -158,8 +159,8 @@ def tile_routed_moe_kernel(tc, xT, w, b, gate, offs, pos1, pos2, out):
         copy_block(sc, late0[:, 1], 1, 0, 1)
         copy_block(sc, high[:, 0], 2, 0, 0)
         copy_block(sc, high[:, 1], 3, 0, 0)
-        copy_block(sc, late0[:, 2], 2, 0, 1)
-        copy_block(sc, late0[:, 3], 3, 0, 1)
+        copy_block(sc, late0b[:, 0], 2, 0, 1)
+        copy_block(sc, late0b[:, 1], 3, 0, 1)
         quantize_w(low, [(0, 0, 0), (1, 0, 0)])
         quantize_w(high, [(2, 0, 0), (3, 0, 0)])
         for e in range(E):
@@ -186,13 +187,14 @@ def tile_routed_moe_kernel(tc, xT, w, b, gate, offs, pos1, pos2, out):
         for e in range(E):
             multiply(e, 1, 0)
             silu(e, 0)
-        quantize_w(late0, [(e, 0, 1) for e in range(E)], after="w_last0")
+        quantize_w(late0, [(0, 0, 1), (1, 0, 1)], after="w_last0")
+        quantize_w(late1, [(0, 1, 1), (1, 1, 1)], after="s210")
         copy_block(ve, last[:, 1], 3, 1, 1)
-        quantize_w(late1, [(0, 1, 1), (1, 1, 1)], after="s310")
+        quantize_w(late0b, [(2, 0, 1), (3, 0, 1)], after="s310")
         quantize_w(last, [(2, 1, 1), (3, 1, 1)])
         y[1] = keep.tile([P, SLOTS], F32, name="y1", tag="bias0")
-        for g in range(PASSES):
-            for e in range(E):
+        for e in range(E):
+            for g in range(PASSES):
                 multiply(e, g, 1)
         for e in range(E):
             silu(e, 1)
@@ -219,16 +221,14 @@ def tile_routed_moe_kernel(tc, xT, w, b, gate, offs, pos1, pos2, out):
             return part
 
         plain_first = fetch(1, 0, 0, T)
-        plain_second = fetch(1, 1, HALF, T)
-        seconds = [gather(1, 1, 0, HALF)]
+        second_part = gather(1, 1)
         first = times_gate(plain_first, 1, 0, 0, T)
-        seconds.append(times_gate(plain_second, 1, 1, HALF, T))
-        total0 = keep.tile([P, T], F32, name="total0", tag="bias0")
+        total0 = keep.tile([P, T], F32, name="total0", tag="bias1")
         for h in range(2):
             columns = slice(h * HALF, (h + 1) * HALF)
             nc.scalar.copy(total0[:, columns], banks[h][:])
             nc.scalar.dma_start(out[:P, columns], total0[:, columns])
         for i, lo in enumerate((0, HALF)):
             total1 = keep.tile([P, HALF], F32, name=f"total1{i}")
-            nc.vector.tensor_tensor(total1[:], first[:, lo : lo + HALF], seconds[i][:], ADD)
+            nc.vector.tensor_tensor(total1[:], first[:, lo : lo + HALF], second_part[:, lo : lo + HALF], ADD)
             nc.sync.dma_start(out[P:, lo : lo + HALF], total1[:])

@@ -24,7 +24,7 @@ SLOTS = E * C
 HALF = T // 2
 WINDOW = 1376
 FIRST_SHARE = 64
-SECOND_SHARE = 160
+SECOND_SHARE = 192
 
 
 def interleave(copy, out, in_):
@@ -83,8 +83,10 @@ def tile_routed_moe_kernel(tc, xT, w, b, gate, offs, pos1, pos2, out):
 
         def copy_x(g, lo, on_vector):
             x_bf = keep.tile([P, HALF, PACK], BF16, name=f"x_bf{g}{lo}", align_bytes=64)
-            if on_vector > 0:
+            if on_vector > 0 and g == 0:
                 interleave(ve, x_bf[:, :on_vector, :], x_raw[g][:, :, lo : lo + on_vector])
+            elif on_vector > 0:
+                nc.gpsimd.tensor_copy(x_bf[:, :on_vector, :], x_raw[g][:, :, lo : lo + on_vector].rearrange("p t n -> p n t"))
             if on_vector < HALF:
                 interleave(sc, x_bf[:, on_vector:, :], x_raw[g][:, :, lo + on_vector : lo + HALF])
             return x_bf
@@ -205,10 +207,10 @@ def tile_routed_moe_kernel(tc, xT, w, b, gate, offs, pos1, pos2, out):
             return part
 
         banks = [psum.tile([P, HALF], F32, name=f"acc{h}0") for h in range(2)]
-        for r in range(2):
-            part = gather(0, r)
-            for h in range(2):
-                nc.tensor.matmul(banks[h][:], identity[:], part[:, h * HALF : (h + 1) * HALF], start=(r == 0), stop=(r == 1))
+        for h in range(2):
+            for r in range(2):
+                part = gather(0, r, h * HALF, (h + 1) * HALF)
+                nc.tensor.matmul(banks[h][:], identity[:], part[:], start=(r == 0), stop=(r == 1))
 
         def fetch(c, r, lo, hi):
             plain = keep.tile([P, hi - lo], F32, name=f"plain{c}{r}{lo}")
@@ -217,12 +219,12 @@ def tile_routed_moe_kernel(tc, xT, w, b, gate, offs, pos1, pos2, out):
 
         def times_gate(plain, c, r, lo, hi):
             part = keep.tile([P, hi - lo], F32, name=f"part{c}{r}{lo}")
-            nc.vector.tensor_tensor(part[:], plain[:], gates[c, r][:, lo:hi], MULT)
+            nc.vector.tensor_tensor(part[:], plain, gates[c, r][:, lo:hi], MULT)
             return part
 
         plain_first = fetch(1, 0, 0, T)
         second_part = gather(1, 1)
-        first = times_gate(plain_first, 1, 0, 0, T)
+        firsts = [times_gate(plain_first[:, lo : lo + HALF], 1, 0, lo, lo + HALF) for lo in (0, HALF)]
         total0 = keep.tile([P, T], F32, name="total0", tag="bias1")
         for h in range(2):
             columns = slice(h * HALF, (h + 1) * HALF)
@@ -230,5 +232,5 @@ def tile_routed_moe_kernel(tc, xT, w, b, gate, offs, pos1, pos2, out):
             nc.scalar.dma_start(out[:P, columns], total0[:, columns])
         for i, lo in enumerate((0, HALF)):
             total1 = keep.tile([P, HALF], F32, name=f"total1{i}")
-            nc.vector.tensor_tensor(total1[:], first[:, lo : lo + HALF], second_part[:, lo : lo + HALF], ADD)
+            nc.vector.tensor_tensor(total1[:], firsts[i][:], second_part[:, lo : lo + HALF], ADD)
             nc.sync.dma_start(out[P:, lo : lo + HALF], total1[:])

@@ -109,7 +109,10 @@ def tile_routed_moe_kernel(tc, xT, w, b, gate, offs, pos1, pos2, out):
 
         def copy_block(copy, to, e, g, c):
             source = w_last[c][:] if (e, g) == (3, 1) else w_raw[e, g][:, :, c * P : (c + 1) * P]
-            interleave(copy, to, source)
+            if copy is gp:
+                copy(to, source.rearrange("p t n -> p n t"))
+            else:
+                interleave(copy, to, source)
 
         def quantize_w(source, pieces, after=None):
             name = "%d%d%d" % pieces[0]
@@ -139,8 +142,7 @@ def tile_routed_moe_kernel(tc, xT, w, b, gate, offs, pos1, pos2, out):
         def silu(e, c):
             nc.scalar.activation(y[c][:, e * C : (e + 1) * C], acc[e, c][:], SILU, bias=bias[c][:, e : e + 1])
 
-        def gp(to, source):
-            nc.gpsimd.tensor_scalar(to, source, 1.0, 0.0, MULT, ADD)
+        gp = nc.gpsimd.tensor_copy
 
         halves = [copy_x(0, 0, HALF), copy_x(0, HALF, FIRST_SHARE)]
         for h in range(2):
@@ -189,6 +191,23 @@ def tile_routed_moe_kernel(tc, xT, w, b, gate, offs, pos1, pos2, out):
         for e in range(E):
             multiply(e, 1, 0)
             silu(e, 0)
+
+        def gather(c, r, lo=0, hi=T):
+            part = keep.tile([P, hi - lo], F32, name=f"part{c}{r}{lo}")
+            nc.vector.tensor_tensor(part[:], y[c][:].indirect(pos_sb[r][:, lo // 16 : hi // 16]), gates[c, r][:, lo:hi], MULT)
+            return part
+
+        def fetch(c, r, lo, hi):
+            plain = keep.tile([P, hi - lo], F32, name=f"plain{c}{r}{lo}")
+            nc.scalar.activation(plain[:], y[c][:].indirect(pos_sb[r][:, lo // 16 : hi // 16]), COPY)
+            return plain
+
+        def times_gate(plain, c, r, lo, hi):
+            part = keep.tile([P, hi - lo], F32, name=f"part{c}{r}{lo}")
+            nc.vector.tensor_tensor(part[:], plain, gates[c, r][:, lo:hi], MULT)
+            return part
+
+        plain_early = fetch(0, 1, HALF, T)
         quantize_w(late0, [(0, 0, 1), (1, 0, 1)], after="w_last0")
         quantize_w(late1, [(0, 1, 1), (1, 1, 1)], after="s210")
         copy_block(ve, last[:, 1], 3, 1, 1)
@@ -201,26 +220,14 @@ def tile_routed_moe_kernel(tc, xT, w, b, gate, offs, pos1, pos2, out):
         for e in range(E):
             silu(e, 1)
 
-        def gather(c, r, lo=0, hi=T):
-            part = keep.tile([P, hi - lo], F32, name=f"part{c}{r}{lo}")
-            nc.vector.tensor_tensor(part[:], y[c][:].indirect(pos_sb[r][:, lo // 16 : hi // 16]), gates[c, r][:, lo:hi], MULT)
-            return part
-
         banks = [psum.tile([P, HALF], F32, name=f"acc{h}0") for h in range(2)]
         for h in range(2):
             for r in range(2):
-                part = gather(0, r, h * HALF, (h + 1) * HALF)
+                if (h, r) == (1, 1):
+                    part = times_gate(plain_early[:], 0, 1, HALF, T)
+                else:
+                    part = gather(0, r, h * HALF, (h + 1) * HALF)
                 nc.tensor.matmul(banks[h][:], identity[:], part[:], start=(r == 0), stop=(r == 1))
-
-        def fetch(c, r, lo, hi):
-            plain = keep.tile([P, hi - lo], F32, name=f"plain{c}{r}{lo}")
-            nc.scalar.activation(plain[:], y[c][:].indirect(pos_sb[r][:, lo // 16 : hi // 16]), COPY)
-            return plain
-
-        def times_gate(plain, c, r, lo, hi):
-            part = keep.tile([P, hi - lo], F32, name=f"part{c}{r}{lo}")
-            nc.vector.tensor_tensor(part[:], plain, gates[c, r][:, lo:hi], MULT)
-            return part
 
         plain_first = fetch(1, 0, 0, T)
         second_part = gather(1, 1)

@@ -25,6 +25,8 @@ HALF = T // 2
 WINDOW = 1376
 FIRST_SHARE = 64
 SECOND_SHARE = 192
+EARLY_FROM = 320
+FILLER = 128
 
 
 def interleave(copy, out, in_):
@@ -46,7 +48,10 @@ def tile_routed_moe_kernel(tc, xT, w, b, gate, offs, pos1, pos2, out):
         w_raw = {(e, g): keep.tile([P, PACK, N], F32, name=f"w_raw{e}{g}", align_bytes=64) for g in range(PASSES) for e in range(E - g)}
         w_last = [keep.tile([P, PACK, P], F32, name=f"w_last{c}", align_bytes=64) for c in range(BLOCKS)]
         bias = [keep.tile([P, E], F32, name=f"bias{c}") for c in range(BLOCKS)]
-        gates = {(c, r): keep.tile([P, T], F32, name=f"gates{c}{r}") for c in range(BLOCKS) for r in range(2)}
+        gates = {(0, r): keep.tile([P, T], F32, name=f"gates0{r}") for r in range(2)}
+        both_gates = keep.tile([P, 2, T], F32, name="gates1")
+        for r in range(2):
+            gates[1, r] = both_gates[:, r, :]
         x_scales = keep.tile([P, WINDOW], U8, name="x_scales", align_bytes=64)
         nc.vector.memset(x_scales[:].bitcast(I32), 0)
         x_codes = [keep.tile([P, WINDOW], I32, name=f"x_codes{g}", align_bytes=64) for g in range(PASSES)]
@@ -75,8 +80,7 @@ def tile_routed_moe_kernel(tc, xT, w, b, gate, offs, pos1, pos2, out):
             nc.sync.dma_start(pos_sb[r][:], pos)
             nc.sync.dma_start(gates[0, r][:], gate[r, :P, :])
         nc.sync.dma_start(bias[1][:], b[P:, :])
-        for r in range(2):
-            nc.sync.dma_start(gates[1, r][:], gate[r, P:, :])
+        nc.sync.dma_start(both_gates[:], gate[:, P:, :].rearrange("r p t -> p r t"))
 
         slot_codes = [keep.tile([P, SLOTS], U32, name="slot_codes0", align_bytes=64)]
         slot_scales = keep.tile([P, SLOTS], U8, name="slot_scales", align_bytes=64)
@@ -147,48 +151,51 @@ def tile_routed_moe_kernel(tc, xT, w, b, gate, offs, pos1, pos2, out):
         halves = [copy_x(0, 0, HALF), copy_x(0, HALF, FIRST_SHARE)]
         for h in range(2):
             quantize_x(0, h * HALF, halves[h])
-        nc.vector.tensor_copy(slot_codes[0][:], x_codes[0][:].bitcast(U32).indirect(offs_sb[:]))
+        cut = SLOTS - FILLER
+        nc.vector.tensor_copy(slot_codes[0][:, :cut], x_codes[0][:].bitcast(U32).indirect(offs_sb[:, : cut // 16]))
         halves = [copy_x(1, 0, 0), copy_x(1, HALF, SECOND_SHARE)]
         for h in range(2):
             quantize_x(1, h * HALF, halves[h])
+        nc.vector.tensor_copy(slot_codes[0][:, cut:], x_codes[0][:].bitcast(U32).indirect(offs_sb[:, cut // 16 :]))
         nc.vector.tensor_copy(slot_scales[:], x_scales[:].indirect(offs_sb[:]))
 
-        late0 = staging("late0", 2, tag=f"x_bf1{HALF}")
-        late0b = staging("late0b", 2)
-        low = staging("low", 2, offset=2048)
-        high = staging("high", 2)
+        late0 = staging("late0", 3, tag=f"x_bf1{HALF}")
+        low = staging("low", 3, offset=2048)
         copy_block(gp, late0[:, 0], 0, 0, 1)
         copy_block(sc, low[:, 0], 0, 0, 0)
         copy_block(sc, low[:, 1], 1, 0, 0)
         copy_block(sc, late0[:, 1], 1, 0, 1)
-        copy_block(sc, high[:, 0], 2, 0, 0)
-        copy_block(sc, high[:, 1], 3, 0, 0)
-        copy_block(sc, late0b[:, 0], 2, 0, 1)
-        copy_block(sc, late0b[:, 1], 3, 0, 1)
-        quantize_w(low, [(0, 0, 0), (1, 0, 0)])
-        quantize_w(high, [(2, 0, 0), (3, 0, 0)])
-        for e in range(E):
-            multiply(e, 0, 0)
-        slot_codes.append(turns.tile([P, SLOTS], U32, name="slot_codes1", offset=4032, align_bytes=64))
+        copy_block(sc, low[:, 2], 2, 0, 0)
+        copy_block(sc, late0[:, 2], 2, 0, 1)
+        quantize_w(low, [(e, 0, 0) for e in range(3)])
+        quantize_w(late0, [(e, 0, 1) for e in range(3)])
+        for c in range(BLOCKS):
+            for e in range(3):
+                multiply(e, 0, c)
+        slot_codes.append(turns.tile([P, SLOTS], U32, name="slot_codes1", offset=5056, align_bytes=64))
         nc.vector.tensor_copy(slot_codes[1][:], x_codes[1][:].bitcast(U32).indirect(offs_sb[:]))
 
         late1 = staging("late1", 2, offset=1024)
-        copy_block(gp, late1[:, 0], 0, 1, 1)
-        second = staging("second", 2)
+        copy_block(gp, late1[:, 0], 3, 0, 1)
+        copy_block(gp, late1[:, 1], 0, 1, 1)
+        second = staging("second", 3)
         s210 = staging("s210", 1)
         last = staging("last", 2)
+        copy_block(sc, second[:, 2], 3, 0, 0)
         copy_block(sc, second[:, 0], 0, 1, 0)
         copy_block(sc, second[:, 1], 1, 1, 0)
-        copy_block(sc, late1[:, 1], 1, 1, 1)
+        copy_block(sc, last[:, 0], 1, 1, 1)
         copy_block(sc, s210[:, 0], 2, 1, 0)
-        copy_block(sc, last[:, 0], 2, 1, 1)
-        quantize_w(second, [(0, 1, 0), (1, 1, 0)])
+        copy_block(sc, last[:, 1], 2, 1, 1)
+        quantize_w(second, [(0, 1, 0), (1, 1, 0), (3, 0, 0)])
         s310 = staging("s310", 1)
         copy_block(ve, s310[:, 0], 3, 1, 0)
         quantize_w(s210, [(2, 1, 0)])
         quantize_w(s310, [(3, 1, 0)])
         y[0] = keep.tile([P, SLOTS], F32, name="y0")
         for e in range(E):
+            if e == 2:
+                multiply(3, 0, 0)
             multiply(e, 1, 0)
             silu(e, 0)
 
@@ -207,31 +214,32 @@ def tile_routed_moe_kernel(tc, xT, w, b, gate, offs, pos1, pos2, out):
             nc.vector.tensor_tensor(part[:], plain, gates[c, r][:, lo:hi], MULT)
             return part
 
-        plain_early = fetch(0, 1, HALF, T)
-        quantize_w(late0, [(0, 0, 1), (1, 0, 1)], after="w_last0")
-        quantize_w(late1, [(0, 1, 1), (1, 1, 1)], after="s210")
-        copy_block(ve, last[:, 1], 3, 1, 1)
-        quantize_w(late0b, [(2, 0, 1), (3, 0, 1)], after="s310")
-        quantize_w(last, [(2, 1, 1), (3, 1, 1)])
+        plain_early = fetch(0, 1, EARLY_FROM, T)
+        quantize_w(late1, [(3, 0, 1), (0, 1, 1)], after="w_last0")
+        s311 = staging("s311", 1)
+        copy_block(ve, s311[:, 0], 3, 1, 1)
+        quantize_w(last, [(1, 1, 1), (2, 1, 1)], after="s310")
+        quantize_w(s311, [(3, 1, 1)])
         y[1] = keep.tile([P, SLOTS], F32, name="y1", tag="bias0")
         for e in range(E):
-            for g in range(PASSES):
+            for g in range(1 if e < 3 else 0, PASSES):
                 multiply(e, g, 1)
         for e in range(E):
             silu(e, 1)
 
         banks = [psum.tile([P, HALF], F32, name=f"acc{h}0") for h in range(2)]
+        second0 = keep.tile([P, T], F32, name="second0")
+        firsts0 = [gather(0, 0, 0, HALF)]
+        nc.vector.tensor_tensor(second0[:, :EARLY_FROM], y[0][:].indirect(pos_sb[1][:, : EARLY_FROM // 16]), gates[0, 1][:, :EARLY_FROM], MULT)
+        firsts0.append(gather(0, 0, HALF, T))
+        nc.vector.tensor_tensor(second0[:, EARLY_FROM:], plain_early[:], gates[0, 1][:, EARLY_FROM:], MULT)
         for h in range(2):
-            for r in range(2):
-                if (h, r) == (1, 1):
-                    part = times_gate(plain_early[:], 0, 1, HALF, T)
-                else:
-                    part = gather(0, r, h * HALF, (h + 1) * HALF)
-                nc.tensor.matmul(banks[h][:], identity[:], part[:], start=(r == 0), stop=(r == 1))
+            nc.tensor.matmul(banks[h][:], identity[:], firsts0[h][:], start=True, stop=False)
+            nc.tensor.matmul(banks[h][:], identity[:], second0[:, h * HALF : (h + 1) * HALF], start=False, stop=True)
 
-        plain_first = fetch(1, 0, 0, T)
+        plain_firsts = [fetch(1, 0, lo, lo + HALF) for lo in (0, HALF)]
         second_part = gather(1, 1)
-        firsts = [times_gate(plain_first[:, lo : lo + HALF], 1, 0, lo, lo + HALF) for lo in (0, HALF)]
+        firsts = [times_gate(plain_firsts[h][:], 1, 0, h * HALF, (h + 1) * HALF) for h in range(2)]
         total0 = keep.tile([P, T], F32, name="total0", tag="bias1")
         for h in range(2):
             columns = slice(h * HALF, (h + 1) * HALF)

@@ -78,8 +78,9 @@ def tile_routed_moe_kernel(tc, xT, w, b, gate, offs, pos1, pos2, out):
         nc.sync.dma_start(w_last[1][:], rows(w[3], 1)[:, :, P:])
         for r, pos in enumerate((pos1, pos2)):
             nc.sync.dma_start(pos_sb[r][:], pos)
+            if r == 1:
+                nc.sync.dma_start(bias[1][:], b[P:, :])
             nc.sync.dma_start(gates[0, r][:], gate[r, :P, :])
-        nc.sync.dma_start(bias[1][:], b[P:, :])
         nc.sync.dma_start(both_gates[:], gate[:, P:, :].rearrange("r p t -> p r t"))
 
         slot_codes = [keep.tile([P, SLOTS], U32, name="slot_codes0", align_bytes=64)]
@@ -137,7 +138,7 @@ def tile_routed_moe_kernel(tc, xT, w, b, gate, offs, pos1, pos2, out):
                 out=acc[e, c][:],
                 lhsT=codes.bitcast(FP8X4),
                 lhsT_scale=scales,
-                rhs=slot_codes[g][:, slots].bitcast(FP8X4),
+                rhs=(slot_codes[0][:, slots] if g == 0 else slot_codes[1][e // 2][:, (e % 2) * C : (e % 2 + 1) * C]).bitcast(FP8X4),
                 rhs_scale=slot_scales[4 * g :, slots],
                 start=(g == 0),
                 stop=(g == PASSES - 1),
@@ -167,21 +168,23 @@ def tile_routed_moe_kernel(tc, xT, w, b, gate, offs, pos1, pos2, out):
         copy_block(sc, late0[:, 1], 1, 0, 1)
         copy_block(sc, low[:, 2], 2, 0, 0)
         copy_block(sc, late0[:, 2], 2, 0, 1)
+        slot_codes.append([keep.tile([P, SLOTS // 2], U32, name="slot_codes10", align_bytes=64)])
+        nc.vector.tensor_copy(slot_codes[1][0][:], x_codes[1][:].bitcast(U32).indirect(offs_sb[:, : SLOTS // 32]))
         quantize_w(low, [(e, 0, 0) for e in range(3)])
         quantize_w(late0, [(e, 0, 1) for e in range(3)])
         for c in range(BLOCKS):
             for e in range(3):
                 multiply(e, 0, c)
-        slot_codes.append(turns.tile([P, SLOTS], U32, name="slot_codes1", offset=5056, align_bytes=64))
-        nc.vector.tensor_copy(slot_codes[1][:], x_codes[1][:].bitcast(U32).indirect(offs_sb[:]))
+        slot_codes[1].append(turns.tile([P, SLOTS // 2], U32, name="slot_codes11", offset=5056, align_bytes=64))
+        nc.vector.tensor_copy(slot_codes[1][1][:], x_codes[1][:].bitcast(U32).indirect(offs_sb[:, SLOTS // 32 :]))
 
-        late1 = staging("late1", 2, offset=1024)
-        copy_block(gp, late1[:, 0], 3, 0, 1)
-        copy_block(gp, late1[:, 1], 0, 1, 1)
+        late1 = staging("late1", 1, offset=2048)
+        copy_block(gp, late1[:, 0], 0, 1, 1)
         second = staging("second", 3)
         s210 = staging("s210", 1)
-        last = staging("last", 2)
+        last = staging("last", 3)
         copy_block(sc, second[:, 2], 3, 0, 0)
+        copy_block(sc, last[:, 2], 3, 0, 1)
         copy_block(sc, second[:, 0], 0, 1, 0)
         copy_block(sc, second[:, 1], 1, 1, 0)
         copy_block(sc, last[:, 0], 1, 1, 1)
@@ -215,10 +218,10 @@ def tile_routed_moe_kernel(tc, xT, w, b, gate, offs, pos1, pos2, out):
             return part
 
         plain_early = fetch(0, 1, EARLY_FROM, T)
-        quantize_w(late1, [(3, 0, 1), (0, 1, 1)], after="w_last0")
+        quantize_w(late1, [(0, 1, 1)], after="w_last0")
         s311 = staging("s311", 1)
         copy_block(ve, s311[:, 0], 3, 1, 1)
-        quantize_w(last, [(1, 1, 1), (2, 1, 1)], after="s310")
+        quantize_w(last, [(1, 1, 1), (2, 1, 1), (3, 0, 1)], after="s310")
         quantize_w(s311, [(3, 1, 1)])
         y[1] = keep.tile([P, SLOTS], F32, name="y1", tag="bias0")
         for e in range(E):

@@ -24,9 +24,8 @@ SLOTS = E * C
 HALF = T // 2
 WINDOW = 1376
 FIRST_SHARE = 64
-SECOND_SHARE = 192
+SECOND_SHARE = 128
 EARLY_FROM = 320
-FILLER = 128
 
 
 def interleave(copy, out, in_):
@@ -152,12 +151,10 @@ def tile_routed_moe_kernel(tc, xT, w, b, gate, offs, pos1, pos2, out):
         halves = [copy_x(0, 0, HALF), copy_x(0, HALF, FIRST_SHARE)]
         for h in range(2):
             quantize_x(0, h * HALF, halves[h])
-        cut = SLOTS - FILLER
-        nc.vector.tensor_copy(slot_codes[0][:, :cut], x_codes[0][:].bitcast(U32).indirect(offs_sb[:, : cut // 16]))
+        nc.vector.tensor_copy(slot_codes[0][:], x_codes[0][:].bitcast(U32).indirect(offs_sb[:]))
         halves = [copy_x(1, 0, 0), copy_x(1, HALF, SECOND_SHARE)]
         for h in range(2):
             quantize_x(1, h * HALF, halves[h])
-        nc.vector.tensor_copy(slot_codes[0][:, cut:], x_codes[0][:].bitcast(U32).indirect(offs_sb[:, cut // 16 :]))
         nc.vector.tensor_copy(slot_scales[:], x_scales[:].indirect(offs_sb[:]))
 
         late0 = staging("late0", 3, tag=f"x_bf1{HALF}")

import concourse.mybir as mybir
from concourse.masks import make_identity

K, T, E, C, N = 1024, 512, 4, 256, 256
FLOPS = 2 * K * N * E * C

F32 = mybir.dt.float32
BF16 = mybir.dt.bfloat16
I32 = mybir.dt.int32
U32 = mybir.dt.uint32
U16 = mybir.dt.uint16
U8 = mybir.dt.uint8
FP8X4 = mybir.dt.float8_e4m3fn_x4
MULT, ADD = mybir.AluOpType.mult, mybir.AluOpType.add
SILU = mybir.ActivationFunctionType.Silu
COPY = mybir.ActivationFunctionType.Copy

P = 128
PACK = 4
K_PASS = P * PACK
PASSES = K // K_PASS
BLOCKS = N // P
SLOTS = E * C
HALF = T // 2
WINDOW = 1376
FIRST_SHARE = 64
SECOND_SHARE = 128
EARLY_FROM = 320


def interleave(copy, out, in_):
    copy(out.rearrange("p (c i) t -> p c t i", i=4), in_.rearrange("p t (c i) -> p c t i", i=4))


def tile_routed_moe_kernel(tc, xT, w, b, gate, offs, pos1, pos2, out):
    nc = tc.nc
    with (
        tc.tile_pool(name="lists", bufs=1) as lists,
        tc.tile_pool(name="keep", bufs=1) as keep,
        tc.tile_pool(name="turns", bufs=1) as turns,
        tc.psum_pool(name="psum", bufs=1) as psum,
    ):
        sc, ve = nc.scalar.copy, nc.vector.tensor_copy
        offs_sb = lists.tile([P, SLOTS // 16], U16, name="offs_sb")
        pos_sb = [lists.tile([P, T // 16], U16, name=f"pos_sb{r}") for r in range(2)]
        x_raw = [keep.tile([P, PACK, T], F32, name=f"x_raw{g}") for g in range(PASSES)]
        w_raw = {(e, g): keep.tile([P, PACK, N], F32, name=f"w_raw{e}{g}", align_bytes=64) for g in range(PASSES) for e in range(E - g)}
        w_last = [keep.tile([P, PACK, P], F32, name=f"w_last{c}", align_bytes=64) for c in range(BLOCKS)]
        bias = [keep.tile([P, E], F32, name=f"bias{c}") for c in range(BLOCKS)]
        gates = {(0, r): keep.tile([P, T], F32, name=f"gates0{r}") for r in range(2)}
        both_gates = keep.tile([P, 2, T], F32, name="gates1")
        for r in range(2):
            gates[1, r] = both_gates[:, r, :]
        x_scales = keep.tile([P, WINDOW], U8, name="x_scales", align_bytes=64)
        nc.vector.memset(x_scales[:].bitcast(I32), 0)
        x_codes = [keep.tile([P, WINDOW], I32, name=f"x_codes{g}", align_bytes=64) for g in range(PASSES)]
        for g in range(PASSES):
            nc.vector.memset(x_codes[g][:, T:], 0)
        warm = keep.tile([P, 1], F32, name="warm")
        nc.gpsimd.memset(warm[:], 0.0)
        warm_out = keep.tile([P, 1], F32, name="warm_out")
        nc.scalar.activation(warm_out[:], warm[:], SILU)
        identity = keep.tile([P, P], F32, name="identity")
        make_identity(nc, identity[:])

        def rows(matrix, g):
            return matrix[g * K_PASS : (g + 1) * K_PASS, :].rearrange("(p j) n -> p j n", j=PACK)

        nc.sync.dma_start(x_raw[0][:], rows(xT, 0))
        nc.sync.dma_start(offs_sb[:], offs)
        nc.sync.dma_start(x_raw[1][:], rows(xT, 1))
        for g in range(PASSES):
            for e in range(E - g):
                nc.sync.dma_start(w_raw[e, g][:], rows(w[e], g))
        nc.sync.dma_start(w_last[0][:], rows(w[3], 1)[:, :, :P])
        nc.sync.dma_start(bias[0][:], b[:P, :])
        nc.sync.dma_start(w_last[1][:], rows(w[3], 1)[:, :, P:])
        for r, pos in enumerate((pos1, pos2)):
            nc.sync.dma_start(pos_sb[r][:], pos)
            if r == 1:
                nc.sync.dma_start(bias[1][:], b[P:, :])
            nc.sync.dma_start(gates[0, r][:], gate[r, :P, :])
        nc.sync.dma_start(both_gates[:], gate[:, P:, :].rearrange("r p t -> p r t"))

        slot_codes = [keep.tile([P, SLOTS], U32, name="slot_codes0", align_bytes=64)]
        slot_scales = keep.tile([P, SLOTS], U8, name="slot_scales", align_bytes=64)

        def copy_x(g, lo, on_vector):
            x_bf = keep.tile([P, HALF, PACK], BF16, name=f"x_bf{g}{lo}", align_bytes=64)
            if on_vector > 0 and g == 0:
                interleave(ve, x_bf[:, :on_vector, :], x_raw[g][:, :, lo : lo + on_vector])
            elif on_vector > 0:
                nc.gpsimd.tensor_copy(x_bf[:, :on_vector, :], x_raw[g][:, :, lo : lo + on_vector].rearrange("p t n -> p n t"))
            if on_vector < HALF:
                interleave(sc, x_bf[:, on_vector:, :], x_raw[g][:, :, lo + on_vector : lo + HALF])
            return x_bf

        def quantize_x(g, lo, x_bf):
            nc.vector.quantize_mx(
                out=x_codes[g][:, lo : lo + HALF].bitcast(FP8X4),
                scales=x_scales[4 * g :, lo : lo + HALF],
                in_=x_bf[:].rearrange("p n t -> p (n t)"),
            )

        acc = {(e, c): psum.tile([P, C], F32, name=f"acc{e}{c}") for e in range(E) for c in range(BLOCKS)}
        y = {}
        w_mx = {}

        def staging(name, pieces, tag=None, offset=None):
            if offset is not None:
                return turns.tile([P, pieces, P, PACK], BF16, name=name, offset=offset, align_bytes=64)
            return keep.tile([P, pieces, P, PACK], BF16, name=name, tag=tag or name, align_bytes=64)

        def copy_block(copy, to, e, g, c):
            source = w_last[c][:] if (e, g) == (3, 1) else w_raw[e, g][:, :, c * P : (c + 1) * P]
            if copy is gp:
                copy(to, source.rearrange("p t n -> p n t"))
            else:
                interleave(copy, to, source)

        def quantize_w(source, pieces, after=None):
            name = "%d%d%d" % pieces[0]
            codes = keep.tile([P, len(pieces), P], U32, name="w_codes" + name, tag=after or "w_codes" + name, align_bytes=64)
            scales = keep.tile([P, len(pieces), P], U8, name="w_scales" + name, align_bytes=64)
            nc.vector.quantize_mx(
                out=codes[:].rearrange("p a n -> p (a n)").bitcast(FP8X4),
                scales=scales[:].rearrange("p a n -> p (a n)"),
                in_=source[:].rearrange("p a n t -> p (a n t)"),
            )
            for j, piece in enumerate(pieces):
                w_mx[piece] = (codes[:, j, :], scales[:, j, :])

        def multiply(e, g, c):
            slots = slice(e * C, (e + 1) * C)
            codes, scales = w_mx[e, g, c]
            nc.tensor.matmul_mx(
                out=acc[e, c][:],
                lhsT=codes.bitcast(FP8X4),
                lhsT_scale=scales,
                rhs=(slot_codes[0][:, slots] if g == 0 else slot_codes[1][e // 2][:, (e % 2) * C : (e % 2 + 1) * C]).bitcast(FP8X4),
                rhs_scale=slot_scales[4 * g :, slots],
                start=(g == 0),
                stop=(g == PASSES - 1),
            )

        def silu(e, c):
            nc.scalar.activation(y[c][:, e * C : (e + 1) * C], acc[e, c][:], SILU, bias=bias[c][:, e : e + 1])

        gp = nc.gpsimd.tensor_copy

        halves = [copy_x(0, 0, HALF), copy_x(0, HALF, FIRST_SHARE)]
        for h in range(2):
            quantize_x(0, h * HALF, halves[h])
        nc.vector.tensor_copy(slot_codes[0][:], x_codes[0][:].bitcast(U32).indirect(offs_sb[:]))
        halves = [copy_x(1, 0, 0), copy_x(1, HALF, SECOND_SHARE)]
        for h in range(2):
            quantize_x(1, h * HALF, halves[h])
        nc.vector.tensor_copy(slot_scales[:], x_scales[:].indirect(offs_sb[:]))

        late0 = staging("late0", 3, tag=f"x_bf1{HALF}")
        low = staging("low", 3, offset=2048)
        copy_block(gp, late0[:, 0], 0, 0, 1)
        copy_block(sc, low[:, 0], 0, 0, 0)
        copy_block(sc, low[:, 1], 1, 0, 0)
        copy_block(sc, late0[:, 1], 1, 0, 1)
        copy_block(sc, low[:, 2], 2, 0, 0)
        copy_block(sc, late0[:, 2], 2, 0, 1)
        slot_codes.append([keep.tile([P, SLOTS // 2], U32, name="slot_codes10", align_bytes=64)])
        nc.vector.tensor_copy(slot_codes[1][0][:], x_codes[1][:].bitcast(U32).indirect(offs_sb[:, : SLOTS // 32]))
        quantize_w(low, [(e, 0, 0) for e in range(3)])
        quantize_w(late0, [(e, 0, 1) for e in range(3)])
        for c in range(BLOCKS):
            for e in range(3):
                multiply(e, 0, c)
        slot_codes[1].append(turns.tile([P, SLOTS // 2], U32, name="slot_codes11", offset=5056, align_bytes=64))
        nc.vector.tensor_copy(slot_codes[1][1][:], x_codes[1][:].bitcast(U32).indirect(offs_sb[:, SLOTS // 32 :]))

        late1 = staging("late1", 1, offset=2048)
        copy_block(gp, late1[:, 0], 0, 1, 1)
        second = staging("second", 3)
        s210 = staging("s210", 1)
        last = staging("last", 3)
        copy_block(sc, second[:, 2], 3, 0, 0)
        copy_block(sc, last[:, 2], 3, 0, 1)
        copy_block(sc, second[:, 0], 0, 1, 0)
        copy_block(sc, second[:, 1], 1, 1, 0)
        copy_block(sc, last[:, 0], 1, 1, 1)
        copy_block(sc, s210[:, 0], 2, 1, 0)
        copy_block(sc, last[:, 1], 2, 1, 1)
        quantize_w(second, [(0, 1, 0), (1, 1, 0), (3, 0, 0)])
        s310 = staging("s310", 1)
        copy_block(ve, s310[:, 0], 3, 1, 0)
        quantize_w(s210, [(2, 1, 0)])
        quantize_w(s310, [(3, 1, 0)])
        y[0] = keep.tile([P, SLOTS], F32, name="y0")
        for e in range(E):
            if e == 2:
                multiply(3, 0, 0)
            multiply(e, 1, 0)
            silu(e, 0)

        def gather(c, r, lo=0, hi=T):
            part = keep.tile([P, hi - lo], F32, name=f"part{c}{r}{lo}")
            nc.vector.tensor_tensor(part[:], y[c][:].indirect(pos_sb[r][:, lo // 16 : hi // 16]), gates[c, r][:, lo:hi], MULT)
            return part

        def fetch(c, r, lo, hi):
            plain = keep.tile([P, hi - lo], F32, name=f"plain{c}{r}{lo}")
            nc.scalar.activation(plain[:], y[c][:].indirect(pos_sb[r][:, lo // 16 : hi // 16]), COPY)
            return plain

        def times_gate(plain, c, r, lo, hi):
            part = keep.tile([P, hi - lo], F32, name=f"part{c}{r}{lo}")
            nc.vector.tensor_tensor(part[:], plain, gates[c, r][:, lo:hi], MULT)
            return part

        plain_early = fetch(0, 1, EARLY_FROM, T)
        quantize_w(late1, [(0, 1, 1)], after="w_last0")
        s311 = staging("s311", 1)
        copy_block(ve, s311[:, 0], 3, 1, 1)
        quantize_w(last, [(1, 1, 1), (2, 1, 1), (3, 0, 1)], after="s310")
        quantize_w(s311, [(3, 1, 1)])
        y[1] = keep.tile([P, SLOTS], F32, name="y1", tag="bias0")
        for e in range(E):
            for g in range(1 if e < 3 else 0, PASSES):
                multiply(e, g, 1)
        for e in range(E):
            silu(e, 1)

        banks = [psum.tile([P, HALF], F32, name=f"acc{h}0") for h in range(2)]
        second0 = keep.tile([P, T], F32, name="second0")
        firsts0 = [gather(0, 0, 0, HALF)]
        nc.vector.tensor_tensor(second0[:, :EARLY_FROM], y[0][:].indirect(pos_sb[1][:, : EARLY_FROM // 16]), gates[0, 1][:, :EARLY_FROM], MULT)
        firsts0.append(gather(0, 0, HALF, T))
        nc.vector.tensor_tensor(second0[:, EARLY_FROM:], plain_early[:], gates[0, 1][:, EARLY_FROM:], MULT)
        for h in range(2):
            nc.tensor.matmul(banks[h][:], identity[:], firsts0[h][:], start=True, stop=False)
            nc.tensor.matmul(banks[h][:], identity[:], second0[:, h * HALF : (h + 1) * HALF], start=False, stop=True)

        plain_firsts = [fetch(1, 0, lo, lo + HALF) for lo in (0, HALF)]
        second_part = gather(1, 1)
        firsts = [times_gate(plain_firsts[h][:], 1, 0, h * HALF, (h + 1) * HALF) for h in range(2)]
        total0 = keep.tile([P, T], F32, name="total0", tag="bias1")
        for h in range(2):
            columns = slice(h * HALF, (h + 1) * HALF)
            nc.scalar.copy(total0[:, columns], banks[h][:])
            nc.scalar.dma_start(out[:P, columns], total0[:, columns])
        for i, lo in enumerate((0, HALF)):
            total1 = keep.tile([P, HALF], F32, name=f"total1{i}")
            nc.vector.tensor_tensor(total1[:], firsts[i][:], second_part[:, lo : lo + HALF], ADD)
            nc.sync.dma_start(out[P:, lo : lo + HALF], total1[:])
